import numpy as np
import ml_dtypes


def mxq(x, axis, fmt="e4m3"):
    dtype, down = {"e4m3": (ml_dtypes.float8_e4m3fn, 7), "e5m2": (ml_dtypes.float8_e5m2, 14)}[fmt]
    v = np.moveaxis(np.asarray(x, np.float32).astype(ml_dtypes.bfloat16).astype(np.float64), axis, -1)
    blocks = v.reshape(v.shape[:-1] + (-1, 32))
    amax = np.abs(blocks).max(-1, keepdims=True)
    byte = np.maximum(np.where(amax > 0, np.frexp(amax)[1] - 1 + 127, 0) - down, 1)
    scale = np.exp2(byte - 127.0)
    codes = (blocks / scale).astype(np.float32).astype(dtype).astype(np.float64)
    return np.moveaxis((codes * scale).reshape(v.shape), -1, axis)


WIDE = False


def mx_kscale(k):
    if not WIDE:
        return np.ones(k)
    levels = np.array([10, -10, 5, -5, 0])
    if k % 512:
        return np.exp2(np.random.permutation(np.resize(levels, k // 32))).repeat(32)
    a = np.empty((k // 512, 16))
    for p in range(k // 512):
        a[p, :8] = np.random.permutation(np.resize(levels, 8))
        for g in range(8):
            far = levels[np.abs(levels - a[p, g]) >= 10]
            a[p, g + 8] = far[np.random.randint(len(far))]
    return np.exp2(a.ravel()).repeat(32)


def f64(x):
    return np.asarray(x).astype(np.float64)


def striped(idx):
    return np.tile(idx.reshape(-1, 16).T, (8, 1)).astype(np.uint16)


def unstriped(offs):
    return offs[:16].T.reshape(-1).astype(np.int64)


E2M1 = np.array([0.0, 0.5, 1.0, 1.5, 2.0, 3.0, 4.0, 6.0, -0.0, -0.5, -1.0, -1.5, -2.0, -3.0, -4.0, -6.0])


def pack_weight(w, fmt):
    k, n = w.shape
    w = f64(np.asarray(w, np.float32).astype(ml_dtypes.bfloat16)).reshape(k // 32, 32, n)
    amax = np.abs(w).max(1)
    if fmt == "e4m3":
        byte = np.frexp(amax)[1] - 1 + 127 - 7
    else:
        mant, ex = np.frexp(amax / 6.0)
        byte = np.where(mant > 0.5, ex, ex - 1) + 127
    byte = np.clip(np.where(amax > 0, byte, 1), 1, 254)
    scaled = (w * np.exp2(127.0 - byte)[:, None, :]).reshape(k, n).astype(np.float32)
    by_word = np.ascontiguousarray(scaled.reshape(k // 512, 128, 4, n).transpose(0, 1, 3, 2))
    if fmt == "e4m3":
        words = by_word.astype(ml_dtypes.float8_e4m3fn).view(np.uint8)
    else:
        c = by_word.astype(ml_dtypes.float4_e2m1fn).view(np.uint8) & 0xF
        words = (c[..., 0::2] | (c[..., 1::2] << 4)).reshape(k // 512, 128, 2 * n)
    return np.ascontiguousarray(words), np.ascontiguousarray(byte.astype(np.uint8).reshape(k // 512, 16, n))


def unpack_weight(words, scales, fmt):
    g, _, n = scales.shape
    words = np.ascontiguousarray(words).reshape(g, 128, n, -1)
    if fmt == "e4m3":
        vals = words.view(ml_dtypes.float8_e4m3fn).astype(np.float64)
    else:
        nib = np.empty((g, 128, n, 4), np.uint8)
        nib[..., 0::2] = words & 0xF
        nib[..., 1::2] = words >> 4
        vals = E2M1[nib]
    vals = vals * np.repeat(np.exp2(scales.astype(np.float64) - 127.0), 8, axis=1)[..., None]
    return vals.transpose(0, 1, 3, 2).reshape(g * 512, n)


def gelu(v):
    return 0.5 * v * (1.0 + np.tanh(np.sqrt(2.0 / np.pi) * (v + 0.044715 * v**3)))


K, D, H, N, T, S = 1024, 512, 512, 256, 2048, 1024

def setup_inputs():
    n = np.random.standard_normal
    s = mx_kscale(K)[:, None]
    sd = mx_kscale(D)[:, None]
    u = mx_kscale(H)[:, None]
    tab_words, tab_scales = pack_weight(n((K, T)) * s, "e4m3")
    tab2_words, tab2_scales = pack_weight(n((K, T)) * s, "e4m3")
    wr_words, wr_scales = pack_weight(n((K, H)) / np.sqrt(K) / s * u.T, "e4m3")
    wd_words, wd_scales = pack_weight(n((H, N)) / np.sqrt(H) / u, "e2m1")
    return {
        "tab_words": tab_words, "tab_scales": tab_scales,
        "tab2_words": tab2_words, "tab2_scales": tab2_scales,
        "offs": striped(np.random.permutation(T)[:S]),
        "offs2": striped(np.random.permutation(T)[:S]),
        "wl": (n((K, H)) / np.sqrt(K) / s * u.T).astype(np.float32),
        "wr_words": wr_words, "wr_scales": wr_scales,
        "x": (n((D, S)) * sd).astype(np.float32),
        "wb": (n((D, H)) / np.sqrt(D) / sd).astype(np.float32),
        "bb": (0.3 * n(H)).astype(np.float32),
        "gain": (np.exp(0.3 * n(H)) * u[:, 0]).astype(np.float32),
        "wd_words": wd_words, "wd_scales": wd_scales,
    }

def reference(tab_words, tab_scales, tab2_words, tab2_scales, offs, offs2, wl, wr_words, wr_scales, x, wb, bb, gain, wd_words, wd_scales):
    v = unpack_weight(tab_words, tab_scales, "e4m3")[:, unstriped(offs)]
    v2 = unpack_weight(tab2_words, tab2_scales, "e4m3")[:, unstriped(offs2)]
    wr = unpack_weight(wr_words, wr_scales, "e4m3")
    wd = unpack_weight(wd_words, wd_scales, "e2m1")
    a = mxq(f64(wl), 0, "e4m3").T @ v
    b = wr.T @ v2
    g = mxq(f64(wb), 0, "e4m3").T @ mxq(f64(x), 0, "e4m3")
    act = f64(gain)[:, None] * np.tanh(g + f64(bb)[:, None])
    h = np.maximum(a, b) - act
    return wd.T @ mxq(h, 0, "e4m3")

@@ -1,0 +1,294 @@
+from contextlib import ExitStack
+
+import concourse.mybir as mybir
+
+K, D, H, N, T, S = 1024, 512, 512, 256, 2048, 1024
+FLOPS = 2 * S * (2 * K * H + D * H + H * N)
+
+F32 = mybir.dt.float32
+BF16 = mybir.dt.bfloat16
+I32 = mybir.dt.int32
+U32 = mybir.dt.uint32
+U16 = mybir.dt.uint16
+U8 = mybir.dt.uint8
+FP8X4 = mybir.dt.float8_e4m3fn_x4
+FP4X4 = mybir.dt.float4_e2m1fn_x4
+ALU = mybir.AluOpType
+ACT = mybir.ActivationFunctionType
+
+P = 128
+PACK = 4
+K_PASS = P * PACK
+QUADS = 4
+QUAD = 32
+BANK = 512
+CHUNK = 256
+CHUNKS = S // CHUNK
+LIST_ROWS = 16
+X_LOADS = [(0, 256), (256, 512), (512, 768), (768, 1024)]
+
+
+def tile_list_stereo_disparity_scores_kernel(
+    tc, tab_words, tab_scales, tab2_words, tab2_scales, offs, offs2, wl, wr_words, wr_scales,
+    x, wb, bb, gain, wd_words, wd_scales, out,
+):
+    nc = tc.nc
+    with ExitStack() as ctx:
+        keep = ctx.enter_context(tc.tile_pool(name="keep", bufs=1))
+        ring = ctx.enter_context(tc.tile_pool(name="ring", bufs=3))
+        psum = ctx.enter_context(tc.psum_pool(name="psum", bufs=1))
+
+        def held(name, shape, dtype):
+            return keep.tile(shape, dtype, name=name, align_bytes=64)
+
+        def load_scale_rows(plane, scales):
+            passes = scales.shape[0]
+            for q in range(QUADS):
+                nc.sync.dma_start(
+                    out=plane[QUAD * q : QUAD * q + 4 * passes, :],
+                    in_=scales[:, 4 * q : 4 * q + 4, :].bitcast(I32),
+                )
+
+        def load_words(words, src):
+            nc.sync.dma_start(out=words, in_=src.rearrange("p t i -> p (t i)").bitcast(I32))
+
+        def load_rows(raw, rows):
+            nc.sync.dma_start(out=raw, in_=rows.rearrange("(p j) c -> p j c", j=PACK))
+
+        left_list = held("left_list", [P, S // LIST_ROWS], U16)
+        right_list = held("right_list", [P, S // LIST_ROWS], U16)
+        left_plane = held("left_plane", [P, T // 4], I32)
+        right_plane = held("right_plane", [P, T // 4], I32)
+        wr_plane_raw = held("wr_plane_raw", [P, H // 4], I32)
+        wd_plane = held("wd_plane", [P, N // 4], I32)
+        left_words = [held("left_words%d" % a, [P, T], I32) for a in range(2)]
+        right_words = [held("right_words%d" % a, [P, T], I32) for a in range(2)]
+        wl_raw = [held("wl_raw%d" % a, [P, PACK, H], F32) for a in range(2)]
+        wb_raw = held("wb_raw", [P, PACK, H], F32)
+        x_raw = [held("x_raw%d" % i, [P, PACK, hi - lo], F32) for i, (lo, hi) in enumerate(X_LOADS)]
+        wr_raw = held("wr_raw", [P, 2, H], I32)
+        wd_codes = held("wd_codes", [P, 2 * N], U8)
+        bias = held("bias", [P, PACK], F32)
+        gains = held("gains", [P, PACK], F32)
+        warm = held("warm", [P, 8], F32)
+
+        for plane in (left_plane, right_plane, wr_plane_raw, wd_plane):
+            nc.vector.memset(plane[:], 0)
+        nc.gpsimd.memset(warm[:, 0:1], 0.0)
+        nc.scalar.activation(out=warm[:, 4:5], in_=warm[:, 0:1], func=ACT.Tanh)
+
+        nc.sync.dma_start(left_list[:], offs)
+        nc.sync.dma_start(right_list[:], offs2)
+        load_scale_rows(left_plane, tab_scales)
+        load_words(left_words[0][:], tab_words[0])
+        load_rows(wl_raw[0][:], wl[0:K_PASS, :])
+        load_scale_rows(right_plane, tab2_scales)
+        load_rows(wl_raw[1][:], wl[K_PASS : 2 * K_PASS, :])
+        load_words(left_words[1][:], tab_words[1])
+        load_words(right_words[0][:], tab2_words[0])
+        load_scale_rows(wr_plane_raw, wr_scales)
+        nc.sync.dma_start(out=wr_raw[:], in_=wr_words.rearrange("a p c i -> p a (c i)").bitcast(I32))
+        load_rows(wb_raw[:], wb)
+        load_words(right_words[1][:], tab2_words[1])
+        nc.sync.dma_start(out=bias[:], in_=bb.rearrange("(p t) -> p t", t=PACK))
+        nc.sync.dma_start(out=gains[:], in_=gain.rearrange("(p t) -> p t", t=PACK))
+        lo, hi = X_LOADS[0]
+        load_rows(x_raw[0][:], x[:, lo:hi])
+        load_scale_rows(wd_plane, wd_scales)
+        nc.sync.dma_start(out=wd_codes[:].bitcast(I32), in_=wd_words[0].bitcast(I32))
+        for i in range(1, len(X_LOADS)):
+            lo, hi = X_LOADS[i]
+            load_rows(x_raw[i][:], x[:, lo:hi])
+
+        def gather(dst, window, offsets, lo, hi):
+            nc.vector.tensor_copy(dst[:, lo:hi], window.indirect(offsets[:, lo // LIST_ROWS : hi // LIST_ROWS]))
+
+        def round_weight(name, raw, copy):
+            rounded = held(name, [P, PACK, P, PACK], BF16)
+            copy(
+                out=rounded[:].rearrange("p t m j -> p m j t"),
+                in_=raw[:].rearrange("p j (m t) -> p m j t", t=PACK),
+            )
+            return rounded
+
+        def quantize(name, pool, rounded, width):
+            codes = pool.tile([P, width], U32, name=name + "_codes", align_bytes=64)
+            plane = pool.tile([P, width], U8, name=name + "_plane", align_bytes=64)
+            nc.vector.quantize_mx(out=codes[:].bitcast(FP8X4), scales=plane[:], in_=rounded)
+            return codes, plane
+
+        v_plane = held("v_plane", [P, S], U8)
+        v2_plane = held("v2_plane", [P, S], U8)
+        v_words = [held("v_words%d" % a, [P, S], U32) for a in range(2)]
+        v2_words = [held("v2_words%d" % a, [P, S], U32) for a in range(2)]
+
+        bank_bufs = {"b": 4, "g": 2, "o": 2}
+
+        def new_bank(tag, shape):
+            return psum.tile(shape, F32, name=tag + "_bank", tag=tag, bufs=bank_bufs[tag])
+
+        def flat(rounded):
+            return rounded[:].rearrange("p t m j -> p (t m j)")
+
+        a_banks = {}
+
+        def left_pass(a, codes, plane):
+            for n, tag in enumerate("bbbbggoo"):
+                half, t = divmod(n, PACK)
+                cols = slice(half * BANK, (half + 1) * BANK)
+                if a == 0:
+                    a_banks[n] = new_bank(tag, [P, BANK])
+                nc.tensor.matmul_mx(
+                    out=a_banks[n][:],
+                    lhsT=codes[:, t * P : (t + 1) * P].bitcast(FP8X4),
+                    lhsT_scale=plane[:, t * P : (t + 1) * P],
+                    rhs=v_words[a][:, cols].bitcast(FP8X4),
+                    rhs_scale=v_plane[4 * a :, cols],
+                    start=(a == 0),
+                    stop=(a == 1),
+                )
+                if a == 1:
+                    nc.scalar.copy(out=a_sb[:, t, cols], in_=a_banks[n][:])
+
+        a_sb = held("a_sb", [P, PACK, S], F32)
+        gather(v_plane, left_plane[:].bitcast(U8), left_list, 0, S)
+        gather(v_words[0], left_words[0][:].bitcast(U32), left_list, 0, S)
+        wl_rounded0 = round_weight("wl_rounded0", wl_raw[0], nc.scalar.copy)
+        gather(v2_plane, right_plane[:].bitcast(U8), right_list, 0, S)
+        wl_rounded1 = round_weight("wl_rounded1", wl_raw[1], nc.scalar.copy)
+        left_pass(0, *quantize("wl0", keep, flat(wl_rounded0), H))
+        gather(v_words[1], left_words[1][:].bitcast(U32), left_list, 0, S)
+        left_pass(1, *quantize("wl1", keep, flat(wl_rounded1), H))
+        gather(v2_words[0], right_words[0][:].bitcast(U32), right_list, 0, S)
+
+        wr_codes = held("wr_codes", [P, 2, H], I32)
+        wr_plane = held("wr_plane", [P, H], U8)
+        nc.vector.tensor_copy(
+            out=wr_codes[:].rearrange("p a (t m) -> p a m t", t=PACK),
+            in_=wr_raw[:].rearrange("p a (m t) -> p a m t", t=PACK),
+        )
+        nc.vector.tensor_copy(
+            out=wr_plane[:].rearrange("p (t m) -> p t m", t=PACK),
+            in_=wr_plane_raw[:].bitcast(U8).rearrange("p (m t) -> p t m", t=PACK),
+        )
+        wb_rounded = round_weight("wb_rounded", wb_raw, nc.vector.tensor_copy)
+        gather(v2_words[1], right_words[1][:].bitcast(U32), right_list, 0, 512)
+        wb_codes, wb_plane = quantize("wb", keep, flat(wb_rounded), H)
+        gather(v2_words[1], right_words[1][:].bitcast(U32), right_list, 512, S)
+
+        stronger = {}
+        x_q = {}
+        x_r = {}
+        tanhs = {}
+        h_c = {}
+        act = {}
+        h_q = {}
+
+        def stage_max(c):
+            m = ring.tile([P, PACK, CHUNK], F32, name="m", bufs=4)
+            cols = slice(c * CHUNK, (c + 1) * CHUNK)
+            for half in range(2):
+                bank = new_bank("b", [P, 2, CHUNK])
+                for e in range(2):
+                    t = 2 * half + e
+                    for a in range(2):
+                        nc.tensor.matmul_mx(
+                            out=bank[:, e, :],
+                            lhsT=wr_codes[:, a, t * P : (t + 1) * P].bitcast(FP8X4),
+                            lhsT_scale=wr_plane[4 * a :, t * P : (t + 1) * P],
+                            rhs=v2_words[a][:, cols].bitcast(FP8X4),
+                            rhs_scale=v2_plane[4 * a :, cols],
+                            start=(a == 0),
+                            stop=(a == 1),
+                        )
+                nc.vector.tensor_tensor(
+                    out=m[:, 2 * half : 2 * half + 2, :], in0=bank[:], in1=a_sb[:, 2 * half : 2 * half + 2, cols],
+                    op=ALU.max,
+                )
+            stronger[c] = m
+
+        def stage_x(c):
+            rounded = ring.tile([P, CHUNK, PACK], BF16, name="x_rounded", align_bytes=64, bufs=4)
+            nc.scalar.copy(
+                out=rounded[:].rearrange("p (c i) j -> p c j i", i=4),
+                in_=x_raw[c][:].rearrange("p j (c i) -> p c j i", i=4),
+            )
+            x_r[c] = rounded
+
+        def stage_xq(c):
+            x_q[c] = quantize("x", ring, x_r[c][:].rearrange("p n j -> p (n j)"), CHUNK)
+
+        def stage_tanh(c):
+            codes, plane = x_q[c]
+            th = ring.tile([P, PACK, CHUNK], F32, name="th")
+            scaled = ring.tile([P, PACK, CHUNK], F32, name="scaled")
+            for half in range(2):
+                bank = new_bank("g", [P, 2, CHUNK])
+                for e in range(2):
+                    t = 2 * half + e
+                    nc.tensor.matmul_mx(
+                        out=bank[:, e, :],
+                        lhsT=wb_codes[:, t * P : (t + 1) * P].bitcast(FP8X4),
+                        lhsT_scale=wb_plane[:, t * P : (t + 1) * P],
+                        rhs=codes[:].bitcast(FP8X4),
+                        rhs_scale=plane[:],
+                        start=True,
+                        stop=True,
+                    )
+                for e in range(2):
+                    t = 2 * half + e
+                    nc.scalar.activation(out=th[:, t, :], in_=bank[:, e, :], func=ACT.Tanh, bias=bias[:, t : t + 1])
+            for t in range(2, 4):
+                nc.scalar.activation(out=scaled[:, t, :], in_=th[:, t, :], func=ACT.Copy, scale=gains[:, t : t + 1])
+            tanhs[c] = th
+            act[c] = scaled
+
+        def stage_gain(c):
+            for t in range(2):
+                nc.vector.tensor_scalar(
+                    out=act[c][:, t, :], in0=tanhs[c][:, t, :], scalar1=gains[:, t : t + 1], scalar2=None,
+                    op0=ALU.mult,
+                )
+
+        def stage_h(c):
+            h = ring.tile([P, CHUNK, PACK], BF16, name="h", align_bytes=64)
+            nc.vector.tensor_tensor(
+                out=h[:].rearrange("p (c i) j -> p c j i", i=4),
+                in0=stronger[c][:].rearrange("p j (c i) -> p c j i", i=4),
+                in1=act[c][:].rearrange("p j (c i) -> p c j i", i=4),
+                op=ALU.subtract,
+            )
+            h_q[c] = h
+
+        def stage_hq(c):
+            h_c[c] = quantize("h", ring, h_q[c][:].rearrange("p n j -> p (n j)"), CHUNK)
+
+        def stage_out(c):
+            codes, plane = h_c[c]
+            bank = new_bank("o", [P, 2, CHUNK])
+            for u in range(2):
+                nc.tensor.matmul_mx(
+                    out=bank[:, u, :],
+                    lhsT=wd_codes[:, 2 * P * u : 2 * P * (u + 1)].bitcast(FP4X4),
+                    lhsT_scale=wd_plane[:].bitcast(U8)[:, P * u : P * (u + 1)],
+                    rhs=codes[:].bitcast(FP8X4),
+                    rhs_scale=plane[:],
+                    start=True,
+                    stop=True,
+                )
+            scores = ring.tile([P, 2, CHUNK], F32, name="scores")
+            nc.scalar.copy(out=scores[:], in_=bank[:])
+            nc.sync.dma_start(
+                out=out.rearrange("(u p) s -> p u s", p=P)[:, :, c * CHUNK : (c + 1) * CHUNK], in_=scores[:]
+            )
+
+        order = [
+            (stage_x, 0), (stage_xq, 0), (stage_x, 1), (stage_max, 0), (stage_tanh, 0), (stage_xq, 1),
+            (stage_max, 1), (stage_x, 2), (stage_gain, 0), (stage_xq, 2), (stage_tanh, 1), (stage_h, 0),
+            (stage_max, 2), (stage_hq, 0), (stage_x, 3), (stage_gain, 1), (stage_xq, 3), (stage_tanh, 2),
+            (stage_h, 1), (stage_out, 0), (stage_max, 3), (stage_hq, 1), (stage_tanh, 3), (stage_gain, 2),
+            (stage_out, 1), (stage_h, 2), (stage_gain, 3), (stage_hq, 2), (stage_h, 3), (stage_out, 2),
+            (stage_hq, 3), (stage_out, 3),
+        ]
+        for stage, c in order:
+            stage(c)

@@ -19,13 +19,23 @@ ACT = mybir.ActivationFunctionType
 P = 128
 PACK = 4
 K_PASS = P * PACK
-QUADS = 4
 QUAD = 32
+QUAD_ROWS = 4
+BYTES_I32 = 4
+LIST_ROWS = 16
 BANK = 512
+HALF = S // 2
 CHUNK = 256
 CHUNKS = S // CHUNK
-LIST_ROWS = 16
-X_LOADS = [(0, 256), (256, 512), (512, 768), (768, 1024)]
+RUN = 4
+PIECES = [(0, 0, CHUNK), (1, 0, CHUNK), (2, 0, CHUNK), (3, 0, CHUNK // 2), (3, CHUNK // 2, CHUNK // 2)]
+VECTOR_GAINS = [3, 3, 4, 4]
+LEFT_FIRST, RIGHT_FIRST, PASS_STEP = 0, 4, 8
+BANKS = {"b": 4, "g": 2, "o": 2}
+A_BANKS = "bbbbggoo"
+X_ROUNDED_TAG = ["share_b", "share_a", "share_c", "share_d"]
+X_CODES_TAG = ["share_c", "share_d", "", ""]
+MAX_TAG = ["", "", "share_b", "share_a"]
 
 
 def tile_list_stereo_disparity_scores_kernel(
@@ -38,127 +48,130 @@ def tile_list_stereo_disparity_scores_kernel(
         ring = ctx.enter_context(tc.tile_pool(name="ring", bufs=3))
         psum = ctx.enter_context(tc.psum_pool(name="psum", bufs=1))
 
-        def held(name, shape, dtype):
-            return keep.tile(shape, dtype, name=name, align_bytes=64)
+        def held(name, shape, dtype, tag=""):
+            return keep.tile(shape, dtype, name=name, tag=tag, align_bytes=64)
 
-        def load_scale_rows(plane, scales):
-            passes = scales.shape[0]
-            for q in range(QUADS):
+        def load_weight_scales(plane, scales):
+            rows = QUAD_ROWS * scales.shape[0]
+            for q in range(P // QUAD):
                 nc.sync.dma_start(
-                    out=plane[QUAD * q : QUAD * q + 4 * passes, :],
-                    in_=scales[:, 4 * q : 4 * q + 4, :].bitcast(I32),
+                    out=plane[QUAD * q : QUAD * q + rows, :],
+                    in_=scales[:, QUAD_ROWS * q : QUAD_ROWS * (q + 1), :].bitcast(I32),
                 )
 
+        def load_table_scales(plane, scales, first):
+            for r in range(QUAD_ROWS):
+                rows = scales[:, r::2, :].rearrange("a w col -> w a col")
+                top = first + r + PASS_STEP * (2 * rows.shape[0] - 1)
+                nc.sync.dma_start(out=plane[first + r : top + 1 : PASS_STEP, :], in_=rows.bitcast(I32))
+
         def load_words(words, src):
-            nc.sync.dma_start(out=words, in_=src.rearrange("p t i -> p (t i)").bitcast(I32))
+            nc.sync.dma_start(out=words, in_=src.rearrange("p col j -> p (col j)").bitcast(I32))
 
         def load_rows(raw, rows):
-            nc.sync.dma_start(out=raw, in_=rows.rearrange("(p j) c -> p j c", j=PACK))
+            nc.sync.dma_start(out=raw, in_=rows.rearrange("(p j) col -> p j col", j=PACK))
 
         left_list = held("left_list", [P, S // LIST_ROWS], U16)
         right_list = held("right_list", [P, S // LIST_ROWS], U16)
-        left_plane = held("left_plane", [P, T // 4], I32)
-        right_plane = held("right_plane", [P, T // 4], I32)
-        wr_plane_raw = held("wr_plane_raw", [P, H // 4], I32)
-        wd_plane = held("wd_plane", [P, N // 4], I32)
+        left_plane = held("left_plane", [P, T // BYTES_I32], I32)
+        right_plane = held("right_plane", [P, T // BYTES_I32], I32)
+        wr_plane_raw = held("wr_plane_raw", [P, H // BYTES_I32], I32)
+        wd_plane = held("wd_plane", [P, N // BYTES_I32], I32)
         left_words = [held("left_words%d" % a, [P, T], I32) for a in range(2)]
         right_words = [held("right_words%d" % a, [P, T], I32) for a in range(2)]
         wl_raw = [held("wl_raw%d" % a, [P, PACK, H], F32) for a in range(2)]
         wb_raw = held("wb_raw", [P, PACK, H], F32)
-        x_raw = [held("x_raw%d" % i, [P, PACK, hi - lo], F32) for i, (lo, hi) in enumerate(X_LOADS)]
+        x_raw = [held("x_raw%d" % half, [P, PACK, HALF], F32) for half in range(2)]
         wr_raw = held("wr_raw", [P, 2, H], I32)
         wd_codes = held("wd_codes", [P, 2 * N], U8)
         bias = held("bias", [P, PACK], F32)
         gains = held("gains", [P, PACK], F32)
-        warm = held("warm", [P, 8], F32)
 
         for plane in (left_plane, right_plane, wr_plane_raw, wd_plane):
             nc.vector.memset(plane[:], 0)
-        nc.gpsimd.memset(warm[:, 0:1], 0.0)
-        nc.scalar.activation(out=warm[:, 4:5], in_=warm[:, 0:1], func=ACT.Tanh)
 
         nc.sync.dma_start(left_list[:], offs)
-        nc.sync.dma_start(right_list[:], offs2)
-        load_scale_rows(left_plane, tab_scales)
         load_words(left_words[0][:], tab_words[0])
+        load_table_scales(left_plane, tab_scales, LEFT_FIRST)
+        nc.sync.dma_start(right_list[:], offs2)
         load_rows(wl_raw[0][:], wl[0:K_PASS, :])
-        load_scale_rows(right_plane, tab2_scales)
+        load_table_scales(right_plane, tab2_scales, RIGHT_FIRST)
         load_rows(wl_raw[1][:], wl[K_PASS : 2 * K_PASS, :])
         load_words(left_words[1][:], tab_words[1])
         load_words(right_words[0][:], tab2_words[0])
-        load_scale_rows(wr_plane_raw, wr_scales)
-        nc.sync.dma_start(out=wr_raw[:], in_=wr_words.rearrange("a p c i -> p a (c i)").bitcast(I32))
-        load_rows(wb_raw[:], wb)
+        nc.sync.dma_start(out=wr_raw[:], in_=wr_words.rearrange("a p col j -> p a (col j)").bitcast(I32))
+        load_weight_scales(wr_plane_raw, wr_scales)
         load_words(right_words[1][:], tab2_words[1])
+        load_rows(wb_raw[:], wb)
+        load_rows(x_raw[0][:], x[:, 0:HALF])
         nc.sync.dma_start(out=bias[:], in_=bb.rearrange("(p t) -> p t", t=PACK))
         nc.sync.dma_start(out=gains[:], in_=gain.rearrange("(p t) -> p t", t=PACK))
-        lo, hi = X_LOADS[0]
-        load_rows(x_raw[0][:], x[:, lo:hi])
-        load_scale_rows(wd_plane, wd_scales)
+        load_rows(x_raw[1][:], x[:, HALF:S])
+        load_weight_scales(wd_plane, wd_scales)
         nc.sync.dma_start(out=wd_codes[:].bitcast(I32), in_=wd_words[0].bitcast(I32))
-        for i in range(1, len(X_LOADS)):
-            lo, hi = X_LOADS[i]
-            load_rows(x_raw[i][:], x[:, lo:hi])
 
         def gather(dst, window, offsets, lo, hi):
             nc.vector.tensor_copy(dst[:, lo:hi], window.indirect(offsets[:, lo // LIST_ROWS : hi // LIST_ROWS]))
 
-        def round_weight(name, raw, copy):
-            rounded = held(name, [P, PACK, P, PACK], BF16)
-            copy(
+        def round_weight(name, raw, tag=""):
+            rounded = held(name, [P, PACK, P, PACK], BF16, tag)
+            nc.scalar.activation(
                 out=rounded[:].rearrange("p t m j -> p m j t"),
                 in_=raw[:].rearrange("p j (m t) -> p m j t", t=PACK),
+                func=ACT.Copy,
             )
-            return rounded
+            return rounded[:].rearrange("p t m j -> p (t m j)")
 
-        def quantize(name, pool, rounded, width):
-            codes = pool.tile([P, width], U32, name=name + "_codes", align_bytes=64)
-            plane = pool.tile([P, width], U8, name=name + "_plane", align_bytes=64)
+        def quantize(name, pool, rounded, codes_tag="", plane_tag=""):
+            width = rounded.shape[1] // PACK
+            codes = pool.tile([P, width], U32, name=name + "_codes", tag=codes_tag, align_bytes=64)
+            plane = pool.tile([P, width], U8, name=name + "_plane", tag=plane_tag, align_bytes=64)
             nc.vector.quantize_mx(out=codes[:].bitcast(FP8X4), scales=plane[:], in_=rounded)
             return codes, plane
+
+        def new_bank(use, shape):
+            return psum.tile(shape, F32, name=use + "_bank", tag=use, bufs=BANKS[use])
+
+        def lane(t):
+            return slice(t * P, (t + 1) * P)
 
         v_plane = held("v_plane", [P, S], U8)
         v2_plane = held("v2_plane", [P, S], U8)
         v_words = [held("v_words%d" % a, [P, S], U32) for a in range(2)]
         v2_words = [held("v2_words%d" % a, [P, S], U32) for a in range(2)]
-
-        bank_bufs = {"b": 4, "g": 2, "o": 2}
-
-        def new_bank(tag, shape):
-            return psum.tile(shape, F32, name=tag + "_bank", tag=tag, bufs=bank_bufs[tag])
-
-        def flat(rounded):
-            return rounded[:].rearrange("p t m j -> p (t m j)")
-
+        a_sb = held("a_sb", [P, PACK, S], F32)
         a_banks = {}
 
-        def left_pass(a, codes, plane):
-            for n, tag in enumerate("bbbbggoo"):
-                half, t = divmod(n, PACK)
-                cols = slice(half * BANK, (half + 1) * BANK)
+        def left_pass(a, half, codes, plane):
+            cols = slice(half * HALF, (half + 1) * HALF)
+            for t in range(PACK):
                 if a == 0:
-                    a_banks[n] = new_bank(tag, [P, BANK])
+                    a_banks[half, t] = new_bank(A_BANKS[PACK * half + t], [P, BANK])
                 nc.tensor.matmul_mx(
-                    out=a_banks[n][:],
-                    lhsT=codes[:, t * P : (t + 1) * P].bitcast(FP8X4),
-                    lhsT_scale=plane[:, t * P : (t + 1) * P],
+                    out=a_banks[half, t][:],
+                    lhsT=codes[:, lane(t)].bitcast(FP8X4),
+                    lhsT_scale=plane[:, lane(t)],
                     rhs=v_words[a][:, cols].bitcast(FP8X4),
-                    rhs_scale=v_plane[4 * a :, cols],
+                    rhs_scale=v_plane[LEFT_FIRST + PASS_STEP * a :, cols],
                     start=(a == 0),
                     stop=(a == 1),
                 )
                 if a == 1:
-                    nc.scalar.copy(out=a_sb[:, t, cols], in_=a_banks[n][:])
+                    nc.scalar.copy(out=a_sb[:, t, cols], in_=a_banks[half, t][:])
 
-        a_sb = held("a_sb", [P, PACK, S], F32)
-        gather(v_plane, left_plane[:].bitcast(U8), left_list, 0, S)
         gather(v_words[0], left_words[0][:].bitcast(U32), left_list, 0, S)
-        wl_rounded0 = round_weight("wl_rounded0", wl_raw[0], nc.scalar.copy)
+        gather(v_plane, left_plane[:].bitcast(U8), left_list, 0, S)
+        wl_rounded0 = round_weight("wl_rounded0", wl_raw[0])
         gather(v2_plane, right_plane[:].bitcast(U8), right_list, 0, S)
-        wl_rounded1 = round_weight("wl_rounded1", wl_raw[1], nc.scalar.copy)
-        left_pass(0, *quantize("wl0", keep, flat(wl_rounded0), H))
-        gather(v_words[1], left_words[1][:].bitcast(U32), left_list, 0, S)
-        left_pass(1, *quantize("wl1", keep, flat(wl_rounded1), H))
+        wl_rounded1 = round_weight("wl_rounded1", wl_raw[1])
+        wl_q0 = quantize("wl0", keep, wl_rounded0)
+        left_pass(0, 0, *wl_q0)
+        left_pass(0, 1, *wl_q0)
+        gather(v_words[1], left_words[1][:].bitcast(U32), left_list, 0, HALF)
+        wl_q1 = quantize("wl1", keep, wl_rounded1, "share_a", "share_b")
+        left_pass(1, 0, *wl_q1)
+        gather(v_words[1], left_words[1][:].bitcast(U32), left_list, HALF, S)
+        left_pass(1, 1, *wl_q1)
         gather(v2_words[0], right_words[0][:].bitcast(U32), right_list, 0, S)
 
         wr_codes = held("wr_codes", [P, 2, H], I32)
@@ -171,102 +184,94 @@ def tile_list_stereo_disparity_scores_kernel(
             out=wr_plane[:].rearrange("p (t m) -> p t m", t=PACK),
             in_=wr_plane_raw[:].bitcast(U8).rearrange("p (m t) -> p t m", t=PACK),
         )
-        wb_rounded = round_weight("wb_rounded", wb_raw, nc.vector.tensor_copy)
-        gather(v2_words[1], right_words[1][:].bitcast(U32), right_list, 0, 512)
-        wb_codes, wb_plane = quantize("wb", keep, flat(wb_rounded), H)
-        gather(v2_words[1], right_words[1][:].bitcast(U32), right_list, 512, S)
+        gather(v2_words[1], right_words[1][:].bitcast(U32), right_list, 0, HALF)
+        gather(v2_words[1], right_words[1][:].bitcast(U32), right_list, HALF, S)
+        wb_codes, wb_plane = quantize("wb", keep, round_weight("wb_rounded", wb_raw, "share_a"))
 
-        stronger = {}
-        x_q = {}
-        x_r = {}
-        tanhs = {}
-        h_c = {}
-        act = {}
-        h_q = {}
+        x_q, tanhs, background, stronger, h_rounded, h_q = {}, {}, {}, {}, {}, {}
 
-        def stage_max(c):
-            m = ring.tile([P, PACK, CHUNK], F32, name="m", bufs=4)
-            cols = slice(c * CHUNK, (c + 1) * CHUNK)
-            for half in range(2):
-                bank = new_bank("b", [P, 2, CHUNK])
-                for e in range(2):
-                    t = 2 * half + e
-                    for a in range(2):
-                        nc.tensor.matmul_mx(
-                            out=bank[:, e, :],
-                            lhsT=wr_codes[:, a, t * P : (t + 1) * P].bitcast(FP8X4),
-                            lhsT_scale=wr_plane[4 * a :, t * P : (t + 1) * P],
-                            rhs=v2_words[a][:, cols].bitcast(FP8X4),
-                            rhs_scale=v2_plane[4 * a :, cols],
-                            start=(a == 0),
-                            stop=(a == 1),
-                        )
-                nc.vector.tensor_tensor(
-                    out=m[:, 2 * half : 2 * half + 2, :], in0=bank[:], in1=a_sb[:, 2 * half : 2 * half + 2, cols],
-                    op=ALU.max,
-                )
-            stronger[c] = m
-
-        def stage_x(c):
-            rounded = ring.tile([P, CHUNK, PACK], BF16, name="x_rounded", align_bytes=64, bufs=4)
+        def quantize_x(c):
+            half, at = divmod(c * CHUNK, HALF)
+            rounded = held("x_rounded", [P, CHUNK, PACK], BF16, X_ROUNDED_TAG[c])
             nc.scalar.copy(
-                out=rounded[:].rearrange("p (c i) j -> p c j i", i=4),
-                in_=x_raw[c][:].rearrange("p j (c i) -> p c j i", i=4),
+                out=rounded[:].rearrange("p (run i) j -> p run j i", i=RUN),
+                in_=x_raw[half][:, :, at : at + CHUNK].rearrange("p j (run i) -> p run j i", i=RUN),
             )
-            x_r[c] = rounded
+            x_q[c] = quantize("x%d" % c, keep, rounded[:].rearrange("p col j -> p (col j)"), X_CODES_TAG[c])
 
-        def stage_xq(c):
-            x_q[c] = quantize("x", ring, x_r[c][:].rearrange("p n j -> p (n j)"), CHUNK)
-
-        def stage_tanh(c):
+        def tanh_of_g(c):
             codes, plane = x_q[c]
-            th = ring.tile([P, PACK, CHUNK], F32, name="th")
-            scaled = ring.tile([P, PACK, CHUNK], F32, name="scaled")
-            for half in range(2):
+            tanhs[c] = ring.tile([P, PACK, CHUNK], F32, name="tanhs", bufs=CHUNKS)
+            for pair in range(0, PACK, 2):
                 bank = new_bank("g", [P, 2, CHUNK])
                 for e in range(2):
-                    t = 2 * half + e
                     nc.tensor.matmul_mx(
                         out=bank[:, e, :],
-                        lhsT=wb_codes[:, t * P : (t + 1) * P].bitcast(FP8X4),
-                        lhsT_scale=wb_plane[:, t * P : (t + 1) * P],
+                        lhsT=wb_codes[:, lane(pair + e)].bitcast(FP8X4),
+                        lhsT_scale=wb_plane[:, lane(pair + e)],
                         rhs=codes[:].bitcast(FP8X4),
                         rhs_scale=plane[:],
                         start=True,
                         stop=True,
                     )
                 for e in range(2):
-                    t = 2 * half + e
-                    nc.scalar.activation(out=th[:, t, :], in_=bank[:, e, :], func=ACT.Tanh, bias=bias[:, t : t + 1])
-            for t in range(2, 4):
-                nc.scalar.activation(out=scaled[:, t, :], in_=th[:, t, :], func=ACT.Copy, scale=gains[:, t : t + 1])
-            tanhs[c] = th
-            act[c] = scaled
+                    t = pair + e
+                    nc.scalar.activation(
+                        out=tanhs[c][:, t, :], in_=bank[:, e, :], func=ACT.Tanh, bias=bias[:, t : t + 1]
+                    )
+            background[c] = ring.tile([P, PACK, CHUNK], F32, name="background")
+            for t in range(VECTOR_GAINS[c], PACK):
+                nc.scalar.activation(
+                    out=background[c][:, t, :], in_=tanhs[c][:, t, :], func=ACT.Copy, scale=gains[:, t : t + 1]
+                )
 
-        def stage_gain(c):
-            for t in range(2):
+        def maximum(c):
+            cols = slice(c * CHUNK, (c + 1) * CHUNK)
+            stronger[c] = held("stronger%d" % c, [P, PACK, CHUNK], F32, MAX_TAG[c])
+            for pair in range(0, PACK, 2):
+                bank = new_bank("b", [P, 2, CHUNK])
+                for e in range(2):
+                    for a in range(2):
+                        nc.tensor.matmul_mx(
+                            out=bank[:, e, :],
+                            lhsT=wr_codes[:, a, lane(pair + e)].bitcast(FP8X4),
+                            lhsT_scale=wr_plane[QUAD_ROWS * a :, lane(pair + e)],
+                            rhs=v2_words[a][:, cols].bitcast(FP8X4),
+                            rhs_scale=v2_plane[RIGHT_FIRST + PASS_STEP * a :, cols],
+                            start=(a == 0),
+                            stop=(a == 1),
+                        )
+                nc.vector.tensor_tensor(
+                    out=stronger[c][:, pair : pair + 2, :], in0=bank[:], in1=a_sb[:, pair : pair + 2, cols],
+                    op=ALU.max,
+                )
+
+        def vector_gains(c):
+            for t in range(VECTOR_GAINS[c]):
                 nc.vector.tensor_scalar(
-                    out=act[c][:, t, :], in0=tanhs[c][:, t, :], scalar1=gains[:, t : t + 1], scalar2=None,
+                    out=background[c][:, t, :], in0=tanhs[c][:, t, :], scalar1=gains[:, t : t + 1], scalar2=None,
                     op0=ALU.mult,
                 )
 
-        def stage_h(c):
-            h = ring.tile([P, CHUNK, PACK], BF16, name="h", align_bytes=64)
+        def difference(n):
+            c, at, width = PIECES[n]
+            h_rounded[n] = ring.tile([P, width, PACK], BF16, name="h_rounded", align_bytes=64)
             nc.vector.tensor_tensor(
-                out=h[:].rearrange("p (c i) j -> p c j i", i=4),
-                in0=stronger[c][:].rearrange("p j (c i) -> p c j i", i=4),
-                in1=act[c][:].rearrange("p j (c i) -> p c j i", i=4),
+                out=h_rounded[n][:].rearrange("p (run i) j -> p run j i", i=RUN),
+                in0=stronger[c][:, :, at : at + width].rearrange("p j (run i) -> p run j i", i=RUN),
+                in1=background[c][:, :, at : at + width].rearrange("p j (run i) -> p run j i", i=RUN),
                 op=ALU.subtract,
             )
-            h_q[c] = h
 
-        def stage_hq(c):
-            h_c[c] = quantize("h", ring, h_q[c][:].rearrange("p n j -> p (n j)"), CHUNK)
+        def quantize_h(n):
+            h_q[n] = quantize("h", ring, h_rounded[n][:].rearrange("p col j -> p (col j)"))
 
-        def stage_out(c):
-            codes, plane = h_c[c]
-            bank = new_bank("o", [P, 2, CHUNK])
-            for u in range(2):
+        def scores(n):
+            c, at, width = PIECES[n]
+            lo = c * CHUNK + at
+            codes, plane = h_q[n]
+            bank = new_bank("o", [P, N // P, width])
+            for u in range(N // P):
                 nc.tensor.matmul_mx(
                     out=bank[:, u, :],
                     lhsT=wd_codes[:, 2 * P * u : 2 * P * (u + 1)].bitcast(FP4X4),
@@ -276,19 +281,31 @@ def tile_list_stereo_disparity_scores_kernel(
                     start=True,
                     stop=True,
                 )
-            scores = ring.tile([P, 2, CHUNK], F32, name="scores")
-            nc.scalar.copy(out=scores[:], in_=bank[:])
-            nc.sync.dma_start(
-                out=out.rearrange("(u p) s -> p u s", p=P)[:, :, c * CHUNK : (c + 1) * CHUNK], in_=scores[:]
-            )
+            staged = ring.tile([P, N // P, width], F32, name="staged")
+            if n == len(PIECES) - 1:
+                nc.vector.tensor_copy(out=staged[:], in_=bank[:])
+            else:
+                nc.scalar.copy(out=staged[:], in_=bank[:])
+            nc.sync.dma_start(out=out.rearrange("(u p) s -> p u s", p=P)[:, :, lo : lo + width], in_=staged[:])
 
-        order = [
-            (stage_x, 0), (stage_xq, 0), (stage_x, 1), (stage_max, 0), (stage_tanh, 0), (stage_xq, 1),
-            (stage_max, 1), (stage_x, 2), (stage_gain, 0), (stage_xq, 2), (stage_tanh, 1), (stage_h, 0),
-            (stage_max, 2), (stage_hq, 0), (stage_x, 3), (stage_gain, 1), (stage_xq, 3), (stage_tanh, 2),
-            (stage_h, 1), (stage_out, 0), (stage_max, 3), (stage_hq, 1), (stage_tanh, 3), (stage_gain, 2),
-            (stage_out, 1), (stage_h, 2), (stage_gain, 3), (stage_hq, 2), (stage_h, 3), (stage_out, 2),
-            (stage_hq, 3), (stage_out, 3),
-        ]
-        for stage, c in order:
-            stage(c)
+        last = len(PIECES) - 1
+        quantize_x(0)
+        tanh_of_g(0)
+        quantize_x(1)
+        for n in range(len(PIECES)):
+            if n + 1 < CHUNKS:
+                tanh_of_g(n + 1)
+            if n + 2 < CHUNKS:
+                quantize_x(n + 2)
+            if n >= 3:
+                scores(n - 3)
+            if n < CHUNKS:
+                maximum(n)
+                vector_gains(n)
+            difference(n)
+            if n >= 1:
+                quantize_h(n - 1)
+        scores(last - 2)
+        quantize_h(last)
+        scores(last - 1)
+        scores(last)

@@ -30,7 +30,6 @@ CHUNKS = S // CHUNK
 RUN = 4
 PIECES = [(0, 0, CHUNK), (1, 0, CHUNK), (2, 0, CHUNK), (3, 0, CHUNK // 2), (3, CHUNK // 2, CHUNK // 2)]
 VECTOR_GAINS = [3, 3, 4, 4]
-LEFT_FIRST, RIGHT_FIRST, PASS_STEP = 0, 4, 8
 BANKS = {"b": 4, "g": 2, "o": 2}
 A_BANKS = "bbbbggoo"
 X_ROUNDED_TAG = ["share_b", "share_a", "share_c", "share_d"]
@@ -59,12 +58,6 @@ def tile_list_stereo_disparity_scores_kernel(
                     in_=scales[:, QUAD_ROWS * q : QUAD_ROWS * (q + 1), :].bitcast(I32),
                 )
 
-        def load_table_scales(plane, scales, first):
-            for r in range(QUAD_ROWS):
-                rows = scales[:, r::2, :].rearrange("a w col -> w a col")
-                top = first + r + PASS_STEP * (2 * rows.shape[0] - 1)
-                nc.sync.dma_start(out=plane[first + r : top + 1 : PASS_STEP, :], in_=rows.bitcast(I32))
-
         def load_words(words, src):
             nc.sync.dma_start(out=words, in_=src.rearrange("p col j -> p (col j)").bitcast(I32))
 
@@ -92,10 +85,10 @@ def tile_list_stereo_disparity_scores_kernel(
 
         nc.sync.dma_start(left_list[:], offs)
         load_words(left_words[0][:], tab_words[0])
-        load_table_scales(left_plane, tab_scales, LEFT_FIRST)
+        load_weight_scales(left_plane, tab_scales)
         nc.sync.dma_start(right_list[:], offs2)
         load_rows(wl_raw[0][:], wl[0:K_PASS, :])
-        load_table_scales(right_plane, tab2_scales, RIGHT_FIRST)
+        load_weight_scales(right_plane, tab2_scales)
         load_rows(wl_raw[1][:], wl[K_PASS : 2 * K_PASS, :])
         load_words(left_words[1][:], tab_words[1])
         load_words(right_words[0][:], tab2_words[0])
@@ -152,7 +145,7 @@ def tile_list_stereo_disparity_scores_kernel(
                     lhsT=codes[:, lane(t)].bitcast(FP8X4),
                     lhsT_scale=plane[:, lane(t)],
                     rhs=v_words[a][:, cols].bitcast(FP8X4),
-                    rhs_scale=v_plane[LEFT_FIRST + PASS_STEP * a :, cols],
+                    rhs_scale=v_plane[QUAD_ROWS * a :, cols],
                     start=(a == 0),
                     stop=(a == 1),
                 )
@@ -237,7 +230,7 @@ def tile_list_stereo_disparity_scores_kernel(
                             lhsT=wr_codes[:, a, lane(pair + e)].bitcast(FP8X4),
                             lhsT_scale=wr_plane[QUAD_ROWS * a :, lane(pair + e)],
                             rhs=v2_words[a][:, cols].bitcast(FP8X4),
-                            rhs_scale=v2_plane[RIGHT_FIRST + PASS_STEP * a :, cols],
+                            rhs_scale=v2_plane[QUAD_ROWS * a :, cols],
                             start=(a == 0),
                             stop=(a == 1),
                         )
@@ -281,7 +274,7 @@ def tile_list_stereo_disparity_scores_kernel(
                     start=True,
                     stop=True,
                 )
-            staged = ring.tile([P, N // P, width], F32, name="staged")
+            staged = ring.tile([P, N // P, width], F32, name="staged", bufs=len(PIECES))
             if n == len(PIECES) - 1:
                 nc.vector.tensor_copy(out=staged[:], in_=bank[:])
             else:

@@ -30,6 +30,8 @@ CHUNKS = S // CHUNK
 RUN = 4
 PIECES = [(0, 0, CHUNK), (1, 0, CHUNK), (2, 0, CHUNK), (3, 0, CHUNK // 2), (3, CHUNK // 2, CHUNK // 2)]
 VECTOR_GAINS = [3, 3, 4, 4]
+LEFT_FIRST, RIGHT_FIRST = 0, 4
+PASS_STEP = 8
 BANKS = {"b": 4, "g": 2, "o": 2}
 A_BANKS = "bbbbggoo"
 X_ROUNDED_TAG = ["share_b", "share_a", "share_c", "share_d"]
@@ -58,6 +60,21 @@ def tile_list_stereo_disparity_scores_kernel(
                     in_=scales[:, QUAD_ROWS * q : QUAD_ROWS * (q + 1), :].bitcast(I32),
                 )
 
+        def load_table_scales(window, scales, first):
+            for e in range(2):
+                rows = scales[:, e::2, :].rearrange("a w col -> w a col")
+                nc.sync.dma_start(out=window[first + e : P : PASS_STEP, :], in_=rows.bitcast(I32))
+
+        def settle_rows(name, gathered, first, tag):
+            words = gathered[:].bitcast(I32)
+            plane = held(name, [P, S // BYTES_I32], I32, tag)
+            nc.vector.tensor_copy(out=plane[:], in_=words)
+            for a in range(2):
+                for e in range(2):
+                    place = first + PASS_STEP * a + 2 + e
+                    nc.scalar.dma_start(out=plane[place:P:QUAD, :], in_=words[place + 14 : P : QUAD, :])
+            return plane[:].bitcast(U8)
+
         def load_words(words, src):
             nc.sync.dma_start(out=words, in_=src.rearrange("p col j -> p (col j)").bitcast(I32))
 
@@ -72,7 +89,7 @@ def tile_list_stereo_disparity_scores_kernel(
         wd_plane = held("wd_plane", [P, N // BYTES_I32], I32)
         left_words = [held("left_words%d" % a, [P, T], I32) for a in range(2)]
         right_words = [held("right_words%d" % a, [P, T], I32) for a in range(2)]
-        wl_raw = [held("wl_raw%d" % a, [P, PACK, H], F32) for a in range(2)]
+        wl_raw = [held("wl_raw%d" % a, [P, PACK, H], F32, "wl_raw%d" % a) for a in range(2)]
         wb_raw = held("wb_raw", [P, PACK, H], F32)
         x_raw = [held("x_raw%d" % half, [P, PACK, HALF], F32) for half in range(2)]
         wr_raw = held("wr_raw", [P, 2, H], I32)
@@ -85,10 +102,10 @@ def tile_list_stereo_disparity_scores_kernel(
 
         nc.sync.dma_start(left_list[:], offs)
         load_words(left_words[0][:], tab_words[0])
-        load_weight_scales(left_plane, tab_scales)
+        load_table_scales(left_plane, tab_scales, LEFT_FIRST)
         nc.sync.dma_start(right_list[:], offs2)
         load_rows(wl_raw[0][:], wl[0:K_PASS, :])
-        load_weight_scales(right_plane, tab2_scales)
+        load_table_scales(right_plane, tab2_scales, RIGHT_FIRST)
         load_rows(wl_raw[1][:], wl[K_PASS : 2 * K_PASS, :])
         load_words(left_words[1][:], tab_words[1])
         load_words(right_words[0][:], tab2_words[0])
@@ -129,7 +146,7 @@ def tile_list_stereo_disparity_scores_kernel(
             return slice(t * P, (t + 1) * P)
 
         v_plane = held("v_plane", [P, S], U8)
-        v2_plane = held("v2_plane", [P, S], U8)
+        planes = []
         v_words = [held("v_words%d" % a, [P, S], U32) for a in range(2)]
         v2_words = [held("v2_words%d" % a, [P, S], U32) for a in range(2)]
         a_sb = held("a_sb", [P, PACK, S], F32)
@@ -145,7 +162,7 @@ def tile_list_stereo_disparity_scores_kernel(
                     lhsT=codes[:, lane(t)].bitcast(FP8X4),
                     lhsT_scale=plane[:, lane(t)],
                     rhs=v_words[a][:, cols].bitcast(FP8X4),
-                    rhs_scale=v_plane[QUAD_ROWS * a :, cols],
+                    rhs_scale=planes[0][LEFT_FIRST + PASS_STEP * a :, cols],
                     start=(a == 0),
                     stop=(a == 1),
                 )
@@ -154,12 +171,15 @@ def tile_list_stereo_disparity_scores_kernel(
 
         gather(v_words[0], left_words[0][:].bitcast(U32), left_list, 0, S)
         gather(v_plane, left_plane[:].bitcast(U8), left_list, 0, S)
-        wl_rounded0 = round_weight("wl_rounded0", wl_raw[0])
-        gather(v2_plane, right_plane[:].bitcast(U8), right_list, 0, S)
-        wl_rounded1 = round_weight("wl_rounded1", wl_raw[1])
+        wl_rounded0 = round_weight("wl_rounded0", wl_raw[0], "share_e")
+        planes.append(settle_rows("left_settled", v_plane, LEFT_FIRST, "wl_raw0"))
         wl_q0 = quantize("wl0", keep, wl_rounded0)
         left_pass(0, 0, *wl_q0)
         left_pass(0, 1, *wl_q0)
+        v2_plane = held("v2_plane", [P, S], U8, "share_e")
+        gather(v2_plane, right_plane[:].bitcast(U8), right_list, 0, S)
+        wl_rounded1 = round_weight("wl_rounded1", wl_raw[1])
+        planes.append(settle_rows("right_settled", v2_plane, RIGHT_FIRST, "wl_raw1"))
         gather(v_words[1], left_words[1][:].bitcast(U32), left_list, 0, HALF)
         wl_q1 = quantize("wl1", keep, wl_rounded1, "share_a", "share_b")
         left_pass(1, 0, *wl_q1)
@@ -230,7 +250,7 @@ def tile_list_stereo_disparity_scores_kernel(
                             lhsT=wr_codes[:, a, lane(pair + e)].bitcast(FP8X4),
                             lhsT_scale=wr_plane[QUAD_ROWS * a :, lane(pair + e)],
                             rhs=v2_words[a][:, cols].bitcast(FP8X4),
-                            rhs_scale=v2_plane[QUAD_ROWS * a :, cols],
+                            rhs_scale=planes[1][RIGHT_FIRST + PASS_STEP * a :, cols],
                             start=(a == 0),
                             stop=(a == 1),
                         )

@@ -65,14 +65,14 @@ def tile_list_stereo_disparity_scores_kernel(
                 rows = scales[:, e::2, :].rearrange("a w col -> w a col")
                 nc.sync.dma_start(out=window[first + e : P : PASS_STEP, :], in_=rows.bitcast(I32))
 
-        def settle_rows(name, gathered, first, tag):
+        def settle_rows(name, gathered, first):
             words = gathered[:].bitcast(I32)
-            plane = held(name, [P, S // BYTES_I32], I32, tag)
+            plane = held(name, [P, S // BYTES_I32], I32, name)
             nc.vector.tensor_copy(out=plane[:], in_=words)
             for a in range(2):
                 for e in range(2):
                     place = first + PASS_STEP * a + 2 + e
-                    nc.scalar.dma_start(out=plane[place:P:QUAD, :], in_=words[place + 14 : P : QUAD, :])
+                    nc.sync.dma_start(out=plane[place:P:QUAD, :], in_=words[place + 14 : P : QUAD, :])
             return plane[:].bitcast(U8)
 
         def load_words(words, src):
@@ -84,41 +84,20 @@ def tile_list_stereo_disparity_scores_kernel(
         left_list = held("left_list", [P, S // LIST_ROWS], U16)
         right_list = held("right_list", [P, S // LIST_ROWS], U16)
         left_plane = held("left_plane", [P, T // BYTES_I32], I32)
-        right_plane = held("right_plane", [P, T // BYTES_I32], I32)
-        wr_plane_raw = held("wr_plane_raw", [P, H // BYTES_I32], I32)
-        wd_plane = held("wd_plane", [P, N // BYTES_I32], I32)
-        left_words = [held("left_words%d" % a, [P, T], I32) for a in range(2)]
-        right_words = [held("right_words%d" % a, [P, T], I32) for a in range(2)]
+        right_plane = held("right_plane", [P, T // BYTES_I32], I32, "right_plane")
+        left_words = [held("left_words0", [P, T], I32, "left_words0")]
         wl_raw = [held("wl_raw%d" % a, [P, PACK, H], F32, "wl_raw%d" % a) for a in range(2)]
-        wb_raw = held("wb_raw", [P, PACK, H], F32)
-        x_raw = [held("x_raw%d" % half, [P, PACK, HALF], F32) for half in range(2)]
-        wr_raw = held("wr_raw", [P, 2, H], I32)
-        wd_codes = held("wd_codes", [P, 2 * N], U8)
-        bias = held("bias", [P, PACK], F32)
-        gains = held("gains", [P, PACK], F32)
 
-        for plane in (left_plane, right_plane, wr_plane_raw, wd_plane):
+        for plane in (left_plane, right_plane):
             nc.vector.memset(plane[:], 0)
 
         nc.sync.dma_start(left_list[:], offs)
-        load_words(left_words[0][:], tab_words[0])
-        load_table_scales(left_plane, tab_scales, LEFT_FIRST)
         nc.sync.dma_start(right_list[:], offs2)
-        load_rows(wl_raw[0][:], wl[0:K_PASS, :])
+        load_table_scales(left_plane, tab_scales, LEFT_FIRST)
         load_table_scales(right_plane, tab2_scales, RIGHT_FIRST)
+        load_rows(wl_raw[0][:], wl[0:K_PASS, :])
+        load_words(left_words[0][:], tab_words[0])
         load_rows(wl_raw[1][:], wl[K_PASS : 2 * K_PASS, :])
-        load_words(left_words[1][:], tab_words[1])
-        load_words(right_words[0][:], tab2_words[0])
-        nc.sync.dma_start(out=wr_raw[:], in_=wr_words.rearrange("a p col j -> p a (col j)").bitcast(I32))
-        load_weight_scales(wr_plane_raw, wr_scales)
-        load_words(right_words[1][:], tab2_words[1])
-        load_rows(wb_raw[:], wb)
-        load_rows(x_raw[0][:], x[:, 0:HALF])
-        nc.sync.dma_start(out=bias[:], in_=bb.rearrange("(p t) -> p t", t=PACK))
-        nc.sync.dma_start(out=gains[:], in_=gain.rearrange("(p t) -> p t", t=PACK))
-        load_rows(x_raw[1][:], x[:, HALF:S])
-        load_weight_scales(wd_plane, wd_scales)
-        nc.sync.dma_start(out=wd_codes[:].bitcast(I32), in_=wd_words[0].bitcast(I32))
 
         def gather(dst, window, offsets, lo, hi):
             nc.vector.tensor_copy(dst[:, lo:hi], window.indirect(offsets[:, lo // LIST_ROWS : hi // LIST_ROWS]))
@@ -145,9 +124,10 @@ def tile_list_stereo_disparity_scores_kernel(
         def lane(t):
             return slice(t * P, (t + 1) * P)
 
-        v_plane = held("v_plane", [P, S], U8)
+        v_plane = held("v_plane", [P, S], U8, "v_plane")
+        v2_plane = held("v2_plane", [P, S], U8, "v2_plane")
         planes = []
-        v_words = [held("v_words%d" % a, [P, S], U32) for a in range(2)]
+        v_words = [held("v_words%d" % a, [P, S], U32, "v_words%d" % a) for a in range(2)]
         v2_words = [held("v2_words%d" % a, [P, S], U32) for a in range(2)]
         a_sb = held("a_sb", [P, PACK, S], F32)
         a_banks = {}
@@ -169,22 +149,48 @@ def tile_list_stereo_disparity_scores_kernel(
                 if a == 1:
                     nc.scalar.copy(out=a_sb[:, t, cols], in_=a_banks[half, t][:])
 
-        gather(v_words[0], left_words[0][:].bitcast(U32), left_list, 0, S)
         gather(v_plane, left_plane[:].bitcast(U8), left_list, 0, S)
-        wl_rounded0 = round_weight("wl_rounded0", wl_raw[0], "share_e")
-        planes.append(settle_rows("left_settled", v_plane, LEFT_FIRST, "wl_raw0"))
-        wl_q0 = quantize("wl0", keep, wl_rounded0)
-        left_pass(0, 0, *wl_q0)
-        left_pass(0, 1, *wl_q0)
-        v2_plane = held("v2_plane", [P, S], U8, "share_e")
+        planes.append(settle_rows("left_settled", v_plane, LEFT_FIRST))
         gather(v2_plane, right_plane[:].bitcast(U8), right_list, 0, S)
-        wl_rounded1 = round_weight("wl_rounded1", wl_raw[1])
-        planes.append(settle_rows("right_settled", v2_plane, RIGHT_FIRST, "wl_raw1"))
+        left_words.append(held("left_words1", [P, T], I32, "right_plane"))
+        load_words(left_words[1][:], tab_words[1])
+        planes.append(settle_rows("right_settled", v2_plane, RIGHT_FIRST))
+        wl_rounded0 = round_weight("wl_rounded0", wl_raw[0], "wl_rounded0")
+        right_words = [held("right_words0", [P, T], I32, "wl_raw0")]
+        load_words(right_words[0][:], tab2_words[0])
+        wl_q0 = quantize("wl0", keep, wl_rounded0, "wl0_codes", "wl0_plane")
+        wr_raw = held("wr_raw", [P, 2, H], I32, "wl_rounded0")
+        nc.sync.dma_start(out=wr_raw[:], in_=wr_words.rearrange("a p col j -> p a (col j)").bitcast(I32))
+        wr_plane_raw = held("wr_plane_raw", [P, H // BYTES_I32], I32, "v_plane")
+        nc.gpsimd.memset(wr_plane_raw[:], 0)
+        load_weight_scales(wr_plane_raw, wr_scales)
+        gather(v_words[0], left_words[0][:].bitcast(U32), left_list, 0, HALF)
+        left_pass(0, 0, *wl_q0)
+        gather(v_words[0], left_words[0][:].bitcast(U32), left_list, HALF, S)
+        left_pass(0, 1, *wl_q0)
+        right_words.append(held("right_words1", [P, T], I32, "left_words0"))
+        load_words(right_words[1][:], tab2_words[1])
+        wl_rounded1 = round_weight("wl_rounded1", wl_raw[1], "wl_rounded1")
+        wb_raw = held("wb_raw", [P, PACK, H], F32, "wl_raw1")
+        load_rows(wb_raw[:], wb)
         gather(v_words[1], left_words[1][:].bitcast(U32), left_list, 0, HALF)
         wl_q1 = quantize("wl1", keep, wl_rounded1, "share_a", "share_b")
+        x_raw = [held("x_raw0", [P, PACK, HALF], F32, "wl_rounded1")]
+        load_rows(x_raw[0][:], x[:, 0:HALF])
+        bias = held("bias", [P, PACK], F32, "wl0_plane")
+        gains = held("gains", [P, PACK], F32, "wl0_codes")
+        nc.sync.dma_start(out=bias[:], in_=bb.rearrange("(p t) -> p t", t=PACK))
+        nc.sync.dma_start(out=gains[:], in_=gain.rearrange("(p t) -> p t", t=PACK))
         left_pass(1, 0, *wl_q1)
         gather(v_words[1], left_words[1][:].bitcast(U32), left_list, HALF, S)
         left_pass(1, 1, *wl_q1)
+        x_raw.append(held("x_raw1", [P, PACK, HALF], F32, "v_words1"))
+        load_rows(x_raw[1][:], x[:, HALF:S])
+        wd_plane = held("wd_plane", [P, N // BYTES_I32], I32, "v_words0")
+        nc.gpsimd.memset(wd_plane[:], 0)
+        load_weight_scales(wd_plane, wd_scales)
+        wd_codes = held("wd_codes", [P, 2 * N], U8, "left_settled")
+        nc.sync.dma_start(out=wd_codes[:].bitcast(I32), in_=wd_words[0].bitcast(I32))
         gather(v2_words[0], right_words[0][:].bitcast(U32), right_list, 0, S)
 
         wr_codes = held("wr_codes", [P, 2, H], I32)

@@ -29,14 +29,16 @@ CHUNK = 256
 CHUNKS = S // CHUNK
 RUN = 4
 PIECES = [(0, 0, CHUNK), (1, 0, CHUNK), (2, 0, CHUNK), (3, 0, CHUNK // 2), (3, CHUNK // 2, CHUNK // 2)]
-VECTOR_GAINS = [3, 3, 4, 4]
-LEFT_FIRST, RIGHT_FIRST = 0, 4
+FIRST = 4
 PASS_STEP = 8
-BANKS = {"b": 4, "g": 2, "o": 2}
-A_BANKS = "bbbbggoo"
-X_ROUNDED_TAG = ["share_b", "share_a", "share_c", "share_d"]
-X_CODES_TAG = ["share_c", "share_d", "", ""]
-MAX_TAG = ["", "", "share_b", "share_a"]
+KIB = 1024
+VECTOR_GAINS = [0, 0, 0, 0]
+G_BANKS = (6, 7)
+O_BANKS = (2, 3)
+
+
+def ab_bank(half, t):
+    return (PACK * half + t) % 6
 
 
 def tile_list_stereo_disparity_scores_kernel(
@@ -46,34 +48,20 @@ def tile_list_stereo_disparity_scores_kernel(
     nc = tc.nc
     with ExitStack() as ctx:
         keep = ctx.enter_context(tc.tile_pool(name="keep", bufs=1))
+        placed = ctx.enter_context(tc.tile_pool(name="placed", bufs=1))
         ring = ctx.enter_context(tc.tile_pool(name="ring", bufs=3))
         psum = ctx.enter_context(tc.psum_pool(name="psum", bufs=1))
 
         def held(name, shape, dtype, tag=""):
             return keep.tile(shape, dtype, name=name, tag=tag, align_bytes=64)
 
-        def load_weight_scales(plane, scales):
-            rows = QUAD_ROWS * scales.shape[0]
-            for q in range(P // QUAD):
-                nc.sync.dma_start(
-                    out=plane[QUAD * q : QUAD * q + rows, :],
-                    in_=scales[:, QUAD_ROWS * q : QUAD_ROWS * (q + 1), :].bitcast(I32),
-                )
+        def at(name, shape, dtype, offset):
+            return placed.tile(shape, dtype, name=name, offset=offset, align_bytes=64)
 
-        def load_table_scales(window, scales, first):
+        def load_scales(window, scales):
             for e in range(2):
                 rows = scales[:, e::2, :].rearrange("a w col -> w a col")
-                nc.sync.dma_start(out=window[first + e : P : PASS_STEP, :], in_=rows.bitcast(I32))
-
-        def settle_rows(name, gathered, first):
-            words = gathered[:].bitcast(I32)
-            plane = held(name, [P, S // BYTES_I32], I32, name)
-            nc.vector.tensor_copy(out=plane[:], in_=words)
-            for a in range(2):
-                for e in range(2):
-                    place = first + PASS_STEP * a + 2 + e
-                    nc.sync.dma_start(out=plane[place:P:QUAD, :], in_=words[place + 14 : P : QUAD, :])
-            return plane[:].bitcast(U8)
+                nc.sync.dma_start(out=window[FIRST + e : P : PASS_STEP, :], in_=rows.bitcast(I32))
 
         def load_words(words, src):
             nc.sync.dma_start(out=words, in_=src.rearrange("p col j -> p (col j)").bitcast(I32))
@@ -81,188 +69,131 @@ def tile_list_stereo_disparity_scores_kernel(
         def load_rows(raw, rows):
             nc.sync.dma_start(out=raw, in_=rows.rearrange("(p j) col -> p j col", j=PACK))
 
-        left_list = held("left_list", [P, S // LIST_ROWS], U16)
-        right_list = held("right_list", [P, S // LIST_ROWS], U16)
-        left_plane = held("left_plane", [P, T // BYTES_I32], I32)
-        right_plane = held("right_plane", [P, T // BYTES_I32], I32, "right_plane")
-        left_words = [held("left_words0", [P, T], I32, "left_words0")]
-        wl_raw = [held("wl_raw%d" % a, [P, PACK, H], F32, "wl_raw%d" % a) for a in range(2)]
-
-        for plane in (left_plane, right_plane):
-            nc.vector.memset(plane[:], 0)
-
-        nc.sync.dma_start(left_list[:], offs)
-        nc.sync.dma_start(right_list[:], offs2)
-        load_table_scales(left_plane, tab_scales, LEFT_FIRST)
-        load_table_scales(right_plane, tab2_scales, RIGHT_FIRST)
-        load_rows(wl_raw[0][:], wl[0:K_PASS, :])
-        load_words(left_words[0][:], tab_words[0])
-        load_rows(wl_raw[1][:], wl[K_PASS : 2 * K_PASS, :])
-
         def gather(dst, window, offsets, lo, hi):
-            nc.vector.tensor_copy(dst[:, lo:hi], window.indirect(offsets[:, lo // LIST_ROWS : hi // LIST_ROWS]))
+            nc.vector.tensor_copy(dst, window.indirect(offsets[:, lo // LIST_ROWS : hi // LIST_ROWS]))
 
-        def round_weight(name, raw, tag=""):
-            rounded = held(name, [P, PACK, P, PACK], BF16, tag)
-            nc.scalar.activation(
-                out=rounded[:].rearrange("p t m j -> p m j t"),
-                in_=raw[:].rearrange("p j (m t) -> p m j t", t=PACK),
-                func=ACT.Copy,
-            )
+        def gather_words(name, window, offsets):
+            words = held(name, [P, S], U32)
+            for lo in (0, HALF):
+                gather(words[:, lo : lo + HALF], window[:].bitcast(U32), offsets, lo, lo + HALF)
+            return words
+
+        def round_weight(name, raw, lanes, on_vector):
+            rounded = held(name, [P, lanes.stop - lanes.start, P, PACK], BF16)
+            dst = rounded[:].rearrange("p t m j -> p m j t")
+            src = raw[:].rearrange("p j (m t) -> p m j t", t=PACK)[:, :, :, lanes]
+            if on_vector:
+                nc.vector.tensor_copy(out=dst, in_=src)
+            else:
+                nc.scalar.activation(out=dst, in_=src, func=ACT.Copy)
             return rounded[:].rearrange("p t m j -> p (t m j)")
 
-        def quantize(name, pool, rounded, codes_tag="", plane_tag=""):
+        def quantize(name, pool, rounded):
             width = rounded.shape[1] // PACK
-            codes = pool.tile([P, width], U32, name=name + "_codes", tag=codes_tag, align_bytes=64)
-            plane = pool.tile([P, width], U8, name=name + "_plane", tag=plane_tag, align_bytes=64)
+            codes = pool.tile([P, width], U32, name=name + "_codes", align_bytes=64)
+            plane = pool.tile([P, width], U8, name=name + "_plane", align_bytes=64)
             nc.vector.quantize_mx(out=codes[:].bitcast(FP8X4), scales=plane[:], in_=rounded)
             return codes, plane
 
-        def new_bank(use, shape):
-            return psum.tile(shape, F32, name=use + "_bank", tag=use, bufs=BANKS[use])
+        def new_bank(number, shape):
+            return psum.tile(shape, F32, name="bank", tag="bank%d" % number)
 
         def lane(t):
             return slice(t * P, (t + 1) * P)
 
-        v_plane = held("v_plane", [P, S], U8, "v_plane")
-        v2_plane = held("v2_plane", [P, S], U8, "v2_plane")
-        planes = []
-        v_words = [held("v_words%d" % a, [P, S], U32, "v_words%d" % a) for a in range(2)]
-        v2_words = [held("v2_words%d" % a, [P, S], U32) for a in range(2)]
-        a_sb = held("a_sb", [P, PACK, S], F32)
-        a_banks = {}
+        left_list = held("left_list", [P, S // LIST_ROWS], U16)
+        right_list = held("right_list", [P, S // LIST_ROWS], U16)
+        right_window = held("right_window", [P, T // BYTES_I32], I32)
+        left_window = held("left_window", [P, T // BYTES_I32], I32)
+        wr_window = at("wr_window", [P, H // BYTES_I32], I32, 8 * KIB - 256)
+        nc.vector.memset(right_window[:], 0)
+        nc.vector.memset(left_window[:], 0)
+        nc.gpsimd.memset(wr_window[:], 0)
 
-        def left_pass(a, half, codes, plane):
-            cols = slice(half * HALF, (half + 1) * HALF)
-            for t in range(PACK):
-                if a == 0:
-                    a_banks[half, t] = new_bank(A_BANKS[PACK * half + t], [P, BANK])
-                nc.tensor.matmul_mx(
-                    out=a_banks[half, t][:],
-                    lhsT=codes[:, lane(t)].bitcast(FP8X4),
-                    lhsT_scale=plane[:, lane(t)],
-                    rhs=v_words[a][:, cols].bitcast(FP8X4),
-                    rhs_scale=planes[0][LEFT_FIRST + PASS_STEP * a :, cols],
-                    start=(a == 0),
-                    stop=(a == 1),
-                )
-                if a == 1:
-                    nc.scalar.copy(out=a_sb[:, t, cols], in_=a_banks[half, t][:])
-
-        gather(v_plane, left_plane[:].bitcast(U8), left_list, 0, S)
-        planes.append(settle_rows("left_settled", v_plane, LEFT_FIRST))
-        gather(v2_plane, right_plane[:].bitcast(U8), right_list, 0, S)
-        left_words.append(held("left_words1", [P, T], I32, "right_plane"))
-        load_words(left_words[1][:], tab_words[1])
-        planes.append(settle_rows("right_settled", v2_plane, RIGHT_FIRST))
-        wl_rounded0 = round_weight("wl_rounded0", wl_raw[0], "wl_rounded0")
-        right_words = [held("right_words0", [P, T], I32, "wl_raw0")]
-        load_words(right_words[0][:], tab2_words[0])
-        wl_q0 = quantize("wl0", keep, wl_rounded0, "wl0_codes", "wl0_plane")
-        wr_raw = held("wr_raw", [P, 2, H], I32, "wl_rounded0")
-        nc.sync.dma_start(out=wr_raw[:], in_=wr_words.rearrange("a p col j -> p a (col j)").bitcast(I32))
-        wr_plane_raw = held("wr_plane_raw", [P, H // BYTES_I32], I32, "v_plane")
-        nc.gpsimd.memset(wr_plane_raw[:], 0)
-        load_weight_scales(wr_plane_raw, wr_scales)
-        gather(v_words[0], left_words[0][:].bitcast(U32), left_list, 0, HALF)
-        left_pass(0, 0, *wl_q0)
-        gather(v_words[0], left_words[0][:].bitcast(U32), left_list, HALF, S)
-        left_pass(0, 1, *wl_q0)
-        right_words.append(held("right_words1", [P, T], I32, "left_words0"))
-        load_words(right_words[1][:], tab2_words[1])
-        wl_rounded1 = round_weight("wl_rounded1", wl_raw[1], "wl_rounded1")
-        wb_raw = held("wb_raw", [P, PACK, H], F32, "wl_raw1")
+        wr_raw = [held("wr_raw%d" % a, [P, H], I32) for a in range(2)]
+        load_words(wr_raw[0][:], wr_words[0])
+        nc.sync.dma_start(right_list[:], offs2)
+        nc.sync.dma_start(left_list[:], offs)
+        load_scales(right_window, tab2_scales)
+        load_scales(left_window, tab_scales)
+        wb_raw = held("wb_raw", [P, PACK, H], F32)
         load_rows(wb_raw[:], wb)
-        gather(v_words[1], left_words[1][:].bitcast(U32), left_list, 0, HALF)
-        wl_q1 = quantize("wl1", keep, wl_rounded1, "share_a", "share_b")
-        x_raw = [held("x_raw0", [P, PACK, HALF], F32, "wl_rounded1")]
+        x_raw = [at("x_raw0", [P, PACK, HALF], F32, 20 * KIB)]
         load_rows(x_raw[0][:], x[:, 0:HALF])
-        bias = held("bias", [P, PACK], F32, "wl0_plane")
-        gains = held("gains", [P, PACK], F32, "wl0_codes")
+        load_scales(wr_window, wr_scales)
+        right_words = [held("right_words%d" % a, [P, T], I32, "right_words%d" % a) for a in range(2)]
+        load_words(right_words[0][:], tab2_words[0])
+        bias = held("bias", [P, PACK], F32)
+        gains = held("gains", [P, PACK], F32)
         nc.sync.dma_start(out=bias[:], in_=bb.rearrange("(p t) -> p t", t=PACK))
         nc.sync.dma_start(out=gains[:], in_=gain.rearrange("(p t) -> p t", t=PACK))
-        left_pass(1, 0, *wl_q1)
-        gather(v_words[1], left_words[1][:].bitcast(U32), left_list, HALF, S)
-        left_pass(1, 1, *wl_q1)
-        x_raw.append(held("x_raw1", [P, PACK, HALF], F32, "v_words1"))
-        load_rows(x_raw[1][:], x[:, HALF:S])
-        wd_plane = held("wd_plane", [P, N // BYTES_I32], I32, "v_words0")
-        nc.gpsimd.memset(wd_plane[:], 0)
-        load_weight_scales(wd_plane, wd_scales)
-        wd_codes = held("wd_codes", [P, 2 * N], U8, "left_settled")
-        nc.sync.dma_start(out=wd_codes[:].bitcast(I32), in_=wd_words[0].bitcast(I32))
-        gather(v2_words[0], right_words[0][:].bitcast(U32), right_list, 0, S)
+        load_words(wr_raw[1][:], wr_words[1])
+        load_words(right_words[1][:], tab2_words[1])
 
-        wr_codes = held("wr_codes", [P, 2, H], I32)
-        wr_plane = held("wr_plane", [P, H], U8)
+        picked = held("picked", [P, 2 * S], U8)
+        gather(picked[:, 0:S], right_window[:].bitcast(U8), right_list, 0, S)
+        gather(picked[:, S : 2 * S], left_window[:].bitcast(U8), left_list, 0, S)
+        settled = held("settled", [P, (2 * S + H) // BYTES_I32], I32)
+        planes = settled[:].bitcast(U8)
+        nc.vector.tensor_copy(out=settled[:, 0 : 2 * S // BYTES_I32], in_=picked[:].bitcast(I32))
         nc.vector.tensor_copy(
-            out=wr_codes[:].rearrange("p a (t m) -> p a m t", t=PACK),
-            in_=wr_raw[:].rearrange("p a (m t) -> p a m t", t=PACK),
+            out=planes[:, 2 * S : 2 * S + H].rearrange("p (t m) -> p t m", t=PACK),
+            in_=wr_window[:].bitcast(U8).rearrange("p (m t) -> p t m", t=PACK),
         )
-        nc.vector.tensor_copy(
-            out=wr_plane[:].rearrange("p (t m) -> p t m", t=PACK),
-            in_=wr_plane_raw[:].bitcast(U8).rearrange("p (m t) -> p t m", t=PACK),
-        )
-        gather(v2_words[1], right_words[1][:].bitcast(U32), right_list, 0, HALF)
-        gather(v2_words[1], right_words[1][:].bitcast(U32), right_list, HALF, S)
-        wb_codes, wb_plane = quantize("wb", keep, round_weight("wb_rounded", wb_raw, "share_a"))
+        for a in range(2):
+            for e in range(2):
+                place = FIRST + PASS_STEP * a + 2 + e
+                nc.sync.dma_start(out=settled[place:P:QUAD, :], in_=settled[place + 14 : P : QUAD, :])
 
-        x_q, tanhs, background, stronger, h_rounded, h_q = {}, {}, {}, {}, {}, {}
+        left_words = [at("left_words0", [P, T], I32, 0), at("left_words1", [P, T], I32, 16 * KIB)]
+        wl_raw = [at("wl_raw0", [P, PACK, H], F32, 8 * KIB), at("wl_raw1", [P, PACK, H], F32, 24 * KIB)]
+        for a in range(2):
+            load_words(left_words[a][:], tab_words[a])
+            load_rows(wl_raw[a][:], wl[a * K_PASS : (a + 1) * K_PASS, :])
+
+        x_rounded, x_q, tanhs, background, stronger, h_rounded, h_q = {}, {}, {}, {}, {}, {}, {}
+
+        def round_x(c):
+            half, lo = divmod(c * CHUNK, HALF)
+            x_rounded[c] = held("x_rounded%d" % c, [P, CHUNK, PACK], BF16)
+            nc.scalar.copy(
+                out=x_rounded[c][:].rearrange("p (run i) j -> p run j i", i=RUN),
+                in_=x_raw[half][:, :, lo : lo + CHUNK].rearrange("p j (run i) -> p run j i", i=RUN),
+            )
 
         def quantize_x(c):
-            half, at = divmod(c * CHUNK, HALF)
-            rounded = held("x_rounded", [P, CHUNK, PACK], BF16, X_ROUNDED_TAG[c])
-            nc.scalar.copy(
-                out=rounded[:].rearrange("p (run i) j -> p run j i", i=RUN),
-                in_=x_raw[half][:, :, at : at + CHUNK].rearrange("p j (run i) -> p run j i", i=RUN),
-            )
-            x_q[c] = quantize("x%d" % c, keep, rounded[:].rearrange("p col j -> p (col j)"), X_CODES_TAG[c])
+            x_q[c] = quantize("x%d" % c, keep, x_rounded[c][:].rearrange("p col j -> p (col j)"))
 
-        def tanh_of_g(c):
+        g_banks = {}
+
+        def g_product(c, pair):
             codes, plane = x_q[c]
-            tanhs[c] = ring.tile([P, PACK, CHUNK], F32, name="tanhs", bufs=CHUNKS)
+            bank = new_bank(G_BANKS[pair // 2], [P, 2, CHUNK])
+            g_banks[c, pair] = bank
+            for e in range(2):
+                nc.tensor.matmul_mx(
+                    out=bank[:, e, :],
+                    lhsT=wb_codes[:, lane(pair + e)].bitcast(FP8X4),
+                    lhsT_scale=wb_plane[:, lane(pair + e)],
+                    rhs=codes[:].bitcast(FP8X4),
+                    rhs_scale=plane[:],
+                    start=True,
+                    stop=True,
+                )
+
+        def activation_of(c):
+            tanhs[c] = ring.tile([P, PACK, CHUNK], F32, name="tanhs", bufs=2)
+            background[c] = held("background%d" % c, [P, PACK, CHUNK], F32)
             for pair in range(0, PACK, 2):
-                bank = new_bank("g", [P, 2, CHUNK])
-                for e in range(2):
-                    nc.tensor.matmul_mx(
-                        out=bank[:, e, :],
-                        lhsT=wb_codes[:, lane(pair + e)].bitcast(FP8X4),
-                        lhsT_scale=wb_plane[:, lane(pair + e)],
-                        rhs=codes[:].bitcast(FP8X4),
-                        rhs_scale=plane[:],
-                        start=True,
-                        stop=True,
-                    )
+                g_product(c, pair)
                 for e in range(2):
                     t = pair + e
                     nc.scalar.activation(
-                        out=tanhs[c][:, t, :], in_=bank[:, e, :], func=ACT.Tanh, bias=bias[:, t : t + 1]
+                        out=tanhs[c][:, t, :], in_=g_banks[c, pair][:, e, :], func=ACT.Tanh, bias=bias[:, t : t + 1]
                     )
-            background[c] = ring.tile([P, PACK, CHUNK], F32, name="background")
             for t in range(VECTOR_GAINS[c], PACK):
                 nc.scalar.activation(
                     out=background[c][:, t, :], in_=tanhs[c][:, t, :], func=ACT.Copy, scale=gains[:, t : t + 1]
-                )
-
-        def maximum(c):
-            cols = slice(c * CHUNK, (c + 1) * CHUNK)
-            stronger[c] = held("stronger%d" % c, [P, PACK, CHUNK], F32, MAX_TAG[c])
-            for pair in range(0, PACK, 2):
-                bank = new_bank("b", [P, 2, CHUNK])
-                for e in range(2):
-                    for a in range(2):
-                        nc.tensor.matmul_mx(
-                            out=bank[:, e, :],
-                            lhsT=wr_codes[:, a, lane(pair + e)].bitcast(FP8X4),
-                            lhsT_scale=wr_plane[QUAD_ROWS * a :, lane(pair + e)],
-                            rhs=v2_words[a][:, cols].bitcast(FP8X4),
-                            rhs_scale=planes[1][RIGHT_FIRST + PASS_STEP * a :, cols],
-                            start=(a == 0),
-                            stop=(a == 1),
-                        )
-                nc.vector.tensor_tensor(
-                    out=stronger[c][:, pair : pair + 2, :], in0=bank[:], in1=a_sb[:, pair : pair + 2, cols],
-                    op=ALU.max,
                 )
 
         def vector_gains(c):
@@ -272,13 +203,98 @@ def tile_list_stereo_disparity_scores_kernel(
                     op0=ALU.mult,
                 )
 
+        wb_codes, wb_plane = quantize("wb", keep, round_weight("wb_rounded", wb_raw, slice(0, PACK), False))
+        round_x(0)
+        round_x(1)
+        quantize_x(0)
+        activation_of(0)
+        vector_gains(0)
+        quantize_x(1)
+        activation_of(1)
+        vector_gains(1)
+        v2_words = [gather_words("v2_words0", right_words[0], right_list)]
+        wr_codes = [held("wr_codes%d" % a, [P, H], I32) for a in range(2)]
+        for a in range(2):
+            nc.gpsimd.tensor_copy(
+                out=wr_codes[a][:].rearrange("p (t m) -> p t m", t=PACK),
+                in_=wr_raw[a][:].rearrange("p (m t) -> p t m", t=PACK),
+            )
+        v2_words.append(gather_words("v2_words1", right_words[1], right_list))
+        x_raw.append(held("x_raw1", [P, PACK, HALF], F32, "right_words1"))
+        load_rows(x_raw[1][:], x[:, HALF:S])
+
+        scalar_lanes = round_weight("wl_s1", wl_raw[1], slice(2, PACK), False)
+        b_sb = held("b_sb", [P, PACK, S], F32)
+        for half in range(2):
+            lo = half * HALF
+            for t in range(PACK):
+                bank = new_bank(PACK * half + t, [P, BANK])
+                for a in range(2):
+                    first = FIRST + PASS_STEP * a
+                    nc.tensor.matmul_mx(
+                        out=bank[:],
+                        lhsT=wr_codes[a][:, lane(t)].bitcast(FP8X4),
+                        lhsT_scale=planes[first:, 2 * S + t * P : 2 * S + (t + 1) * P],
+                        rhs=v2_words[a][:, lo : lo + HALF].bitcast(FP8X4),
+                        rhs_scale=planes[first:, lo : lo + HALF],
+                        start=(a == 0),
+                        stop=(a == 1),
+                    )
+                nc.scalar.copy(out=b_sb[:, t, lo : lo + HALF], in_=bank[:])
+
+        v_words = [gather_words("v_words0", left_words[0], left_list)]
+        wd_codes = at("wd_codes", [P, 2 * N], U8, 0)
+        wd_plane = at("wd_plane", [P, N // BYTES_I32], I32, 2 * N)
+        nc.sync.dma_start(out=wd_codes[:].bitcast(I32), in_=wd_words[0].bitcast(I32))
+        nc.gpsimd.memset(wd_plane[:], 0)
+        for q in range(P // QUAD):
+            nc.sync.dma_start(
+                out=wd_plane[QUAD * q : QUAD * q + QUAD_ROWS, :],
+                in_=wd_scales[0, QUAD_ROWS * q : QUAD_ROWS * (q + 1), :].bitcast(I32),
+            )
+        wl_first = quantize("wl0", keep, round_weight("wl_v0", wl_raw[0], slice(0, PACK), True))
+        a_banks = {}
+
+        def left_pass(a, half, t, codes, plane, column):
+            lo = half * HALF
+            if a == 0:
+                a_banks[half, t] = new_bank(ab_bank(half, t), [P, BANK])
+            nc.tensor.matmul_mx(
+                out=a_banks[half, t][:],
+                lhsT=codes[:, column : column + P].bitcast(FP8X4),
+                lhsT_scale=plane[:, column : column + P],
+                rhs=v_words[a][:, lo : lo + HALF].bitcast(FP8X4),
+                rhs_scale=planes[FIRST + PASS_STEP * a :, S + lo : S + lo + HALF],
+                start=(a == 0),
+                stop=(a == 1),
+            )
+
+        early = [(0, 0), (0, 1), (0, 2), (0, 3), (1, 0), (1, 1)]
+        for half, t in early:
+            left_pass(0, half, t, *wl_first, t * P)
+        v_words.append(gather_words("v_words1", left_words[1], left_list))
+        rounded = [round_weight("wl_v1", wl_raw[1], slice(0, 2), True), scalar_lanes]
+        wl_second = [quantize("wl1_%d" % pair, keep, rounded[pair]) for pair in range(2)]
+
+        def maximum(half, t):
+            lo = half * HALF
+            if (half, t) not in early:
+                left_pass(0, half, t, *wl_first, t * P)
+            left_pass(1, half, t, *wl_second[t // 2], (t % 2) * P)
+            if t == 0:
+                stronger[half] = held("stronger%d" % half, [P, PACK, HALF], F32)
+            nc.vector.tensor_tensor(
+                out=stronger[half][:, t, :], in0=a_banks[half, t][:], in1=b_sb[:, t, lo : lo + HALF], op=ALU.max
+            )
+
         def difference(n):
-            c, at, width = PIECES[n]
+            c, lo, width = PIECES[n]
+            half, first = divmod(c * CHUNK + lo, HALF)
             h_rounded[n] = ring.tile([P, width, PACK], BF16, name="h_rounded", align_bytes=64)
             nc.vector.tensor_tensor(
                 out=h_rounded[n][:].rearrange("p (run i) j -> p run j i", i=RUN),
-                in0=stronger[c][:, :, at : at + width].rearrange("p j (run i) -> p run j i", i=RUN),
-                in1=background[c][:, :, at : at + width].rearrange("p j (run i) -> p run j i", i=RUN),
+                in0=stronger[half][:, :, first : first + width].rearrange("p j (run i) -> p run j i", i=RUN),
+                in1=background[c][:, :, lo : lo + width].rearrange("p j (run i) -> p run j i", i=RUN),
                 op=ALU.subtract,
             )
 
@@ -286,10 +302,10 @@ def tile_list_stereo_disparity_scores_kernel(
             h_q[n] = quantize("h", ring, h_rounded[n][:].rearrange("p col j -> p (col j)"))
 
         def scores(n):
-            c, at, width = PIECES[n]
-            lo = c * CHUNK + at
+            c, lo, width = PIECES[n]
+            first = c * CHUNK + lo
             codes, plane = h_q[n]
-            bank = new_bank("o", [P, N // P, width])
+            bank = new_bank(O_BANKS[n % 2], [P, N // P, width])
             for u in range(N // P):
                 nc.tensor.matmul_mx(
                     out=bank[:, u, :],
@@ -305,26 +321,34 @@ def tile_list_stereo_disparity_scores_kernel(
                 nc.vector.tensor_copy(out=staged[:], in_=bank[:])
             else:
                 nc.scalar.copy(out=staged[:], in_=bank[:])
-            nc.sync.dma_start(out=out.rearrange("(u p) s -> p u s", p=P)[:, :, lo : lo + width], in_=staged[:])
+            nc.sync.dma_start(out=out.rearrange("(u p) s -> p u s", p=P)[:, :, first : first + width], in_=staged[:])
 
-        last = len(PIECES) - 1
-        quantize_x(0)
-        tanh_of_g(0)
-        quantize_x(1)
-        for n in range(len(PIECES)):
-            if n + 1 < CHUNKS:
-                tanh_of_g(n + 1)
-            if n + 2 < CHUNKS:
-                quantize_x(n + 2)
-            if n >= 3:
-                scores(n - 3)
-            if n < CHUNKS:
-                maximum(n)
-                vector_gains(n)
-            difference(n)
-            if n >= 1:
-                quantize_h(n - 1)
-        scores(last - 2)
-        quantize_h(last)
-        scores(last - 1)
-        scores(last)
+        round_x(2)
+        round_x(3)
+        quantize_x(2)
+        activation_of(2)
+        for t in range(PACK):
+            maximum(0, t)
+        quantize_x(3)
+        difference(0)
+        maximum(1, 0)
+        quantize_h(0)
+        scores(0)
+        activation_of(3)
+        difference(1)
+        maximum(1, 1)
+        quantize_h(1)
+        scores(1)
+        maximum(1, 2)
+        maximum(1, 3)
+        vector_gains(2)
+        difference(2)
+        vector_gains(3)
+        difference(3)
+        quantize_h(2)
+        scores(2)
+        difference(4)
+        quantize_h(3)
+        scores(3)
+        quantize_h(4)
+        scores(4)

@@ -154,11 +154,11 @@ def tile_list_stereo_disparity_scores_kernel(
         x_rounded, x_q, tanhs, background, stronger, h_rounded, h_q = {}, {}, {}, {}, {}, {}, {}
 
         def round_x(c):
-            half, lo = divmod(c * CHUNK, HALF)
-            x_rounded[c] = held("x_rounded%d" % c, [P, CHUNK, PACK], BF16)
+            raw = x_raw[0][:, :, c * CHUNK : (c + 1) * CHUNK] if c < 2 else x_late[c - 2][:]
+            x_rounded[c] = held("x_rounded%d" % c, [P, CHUNK, PACK], BF16, "x_rounded%d" % c)
             nc.scalar.copy(
                 out=x_rounded[c][:].rearrange("p (run i) j -> p run j i", i=RUN),
-                in_=x_raw[half][:, :, lo : lo + CHUNK].rearrange("p j (run i) -> p run j i", i=RUN),
+                in_=raw.rearrange("p j (run i) -> p run j i", i=RUN),
             )
 
         def quantize_x(c):
@@ -220,8 +220,8 @@ def tile_list_stereo_disparity_scores_kernel(
                 in_=wr_raw[a][:].rearrange("p (m t) -> p t m", t=PACK),
             )
         v2_words.append(gather_words("v2_words1", right_words[1], right_list))
-        x_raw.append(held("x_raw1", [P, PACK, HALF], F32, "right_words1"))
-        load_rows(x_raw[1][:], x[:, HALF:S])
+        x_late = [held("x_raw2", [P, PACK, CHUNK], F32, "right_words1"), at("x_raw3", [P, PACK, CHUNK], F32, KIB)]
+        load_rows(x_late[0][:], x[:, HALF : HALF + CHUNK])
 
         scalar_lanes = round_weight("wl_s1", wl_raw[1], slice(2, PACK), False)
         b_sb = held("b_sb", [P, PACK, S], F32)
@@ -243,6 +243,7 @@ def tile_list_stereo_disparity_scores_kernel(
                 nc.scalar.copy(out=b_sb[:, t, lo : lo + HALF], in_=bank[:])
 
         v_words = [gather_words("v_words0", left_words[0], left_list)]
+        load_rows(x_late[1][:], x[:, HALF + CHUNK : S])
         wd_codes = at("wd_codes", [P, 2 * N], U8, 0)
         wd_plane = at("wd_plane", [P, N // BYTES_I32], I32, 2 * N)
         nc.sync.dma_start(out=wd_codes[:].bitcast(I32), in_=wd_words[0].bitcast(I32))
@@ -290,8 +291,9 @@ def tile_list_stereo_disparity_scores_kernel(
         def difference(n):
             c, lo, width = PIECES[n]
             half, first = divmod(c * CHUNK + lo, HALF)
-            h_rounded[n] = ring.tile([P, width, PACK], BF16, name="h_rounded", align_bytes=64)
-            nc.vector.tensor_tensor(
+            h_rounded[n] = held("h_rounded%d" % n, [P, width, PACK], BF16, "x_rounded3" if n == 0 else "")
+            engine = nc.gpsimd if n == 0 else nc.vector
+            engine.tensor_tensor(
                 out=h_rounded[n][:].rearrange("p (run i) j -> p run j i", i=RUN),
                 in0=stronger[half][:, :, first : first + width].rearrange("p j (run i) -> p run j i", i=RUN),
                 in1=background[c][:, :, lo : lo + width].rearrange("p j (run i) -> p run j i", i=RUN),
@@ -331,18 +333,16 @@ def tile_list_stereo_disparity_scores_kernel(
             maximum(0, t)
         quantize_x(3)
         difference(0)
-        maximum(1, 0)
-        quantize_h(0)
-        scores(0)
+        for t in range(PACK):
+            maximum(1, t)
         activation_of(3)
         difference(1)
-        maximum(1, 1)
-        quantize_h(1)
-        scores(1)
-        maximum(1, 2)
-        maximum(1, 3)
+        quantize_h(0)
+        scores(0)
         vector_gains(2)
         difference(2)
+        quantize_h(1)
+        scores(1)
         vector_gains(3)
         difference(3)
         quantize_h(2)

@@ -88,9 +88,9 @@ def tile_list_stereo_disparity_scores_kernel(
                 nc.scalar.activation(out=dst, in_=src, func=ACT.Copy)
             return rounded[:].rearrange("p t m j -> p (t m j)")
 
-        def quantize(name, pool, rounded):
+        def quantize(name, pool, rounded, tag=""):
             width = rounded.shape[1] // PACK
-            codes = pool.tile([P, width], U32, name=name + "_codes", align_bytes=64)
+            codes = pool.tile([P, width], U32, name=name + "_codes", tag=tag, align_bytes=64)
             plane = pool.tile([P, width], U8, name=name + "_plane", align_bytes=64)
             nc.vector.quantize_mx(out=codes[:].bitcast(FP8X4), scales=plane[:], in_=rounded)
             return codes, plane
@@ -162,7 +162,7 @@ def tile_list_stereo_disparity_scores_kernel(
             )
 
         def quantize_x(c):
-            x_q[c] = quantize("x%d" % c, keep, x_rounded[c][:].rearrange("p col j -> p (col j)"))
+            x_q[c] = quantize("x%d" % c, keep, x_rounded[c][:].rearrange("p col j -> p (col j)"), "b_sb0" if c == 3 else "")
 
         g_banks = {}
 
@@ -224,7 +224,7 @@ def tile_list_stereo_disparity_scores_kernel(
         load_rows(x_late[0][:], x[:, HALF : HALF + CHUNK])
 
         scalar_lanes = round_weight("wl_s1", wl_raw[1], slice(2, PACK), False)
-        b_sb = held("b_sb", [P, PACK, S], F32)
+        b_sb = [held("b_sb%d" % half, [P, PACK, HALF], F32, "b_sb%d" % half) for half in range(2)]
         for half in range(2):
             lo = half * HALF
             for t in range(PACK):
@@ -240,7 +240,7 @@ def tile_list_stereo_disparity_scores_kernel(
                         start=(a == 0),
                         stop=(a == 1),
                     )
-                nc.scalar.copy(out=b_sb[:, t, lo : lo + HALF], in_=bank[:])
+                nc.scalar.copy(out=b_sb[half][:, t, :], in_=bank[:])
 
         v_words = [gather_words("v_words0", left_words[0], left_list)]
         load_rows(x_late[1][:], x[:, HALF + CHUNK : S])
@@ -256,47 +256,52 @@ def tile_list_stereo_disparity_scores_kernel(
         wl_first = quantize("wl0", keep, round_weight("wl_v0", wl_raw[0], slice(0, PACK), True))
         a_banks = {}
 
-        def left_pass(a, half, t, codes, plane, column):
-            lo = half * HALF
+        def left_pass(a, c, pair, codes, plane, column):
+            lo = c * CHUNK
             if a == 0:
-                a_banks[half, t] = new_bank(ab_bank(half, t), [P, BANK])
-            nc.tensor.matmul_mx(
-                out=a_banks[half, t][:],
-                lhsT=codes[:, column : column + P].bitcast(FP8X4),
-                lhsT_scale=plane[:, column : column + P],
-                rhs=v_words[a][:, lo : lo + HALF].bitcast(FP8X4),
-                rhs_scale=planes[FIRST + PASS_STEP * a :, S + lo : S + lo + HALF],
-                start=(a == 0),
-                stop=(a == 1),
-            )
+                a_banks[c, pair] = new_bank((2 * c + pair) % 6, [P, 2, CHUNK])
+            for e in range(2):
+                cols = slice(column + e * P, column + (e + 1) * P)
+                nc.tensor.matmul_mx(
+                    out=a_banks[c, pair][:, e, :],
+                    lhsT=codes[:, cols].bitcast(FP8X4),
+                    lhsT_scale=plane[:, cols],
+                    rhs=v_words[a][:, lo : lo + CHUNK].bitcast(FP8X4),
+                    rhs_scale=planes[FIRST + PASS_STEP * a :, S + lo : S + lo + CHUNK],
+                    start=(a == 0 and e == 0),
+                    stop=(a == 1 and e == 1),
+                )
 
-        early = [(0, 0), (0, 1), (0, 2), (0, 3), (1, 0), (1, 1)]
-        for half, t in early:
-            left_pass(0, half, t, *wl_first, t * P)
+        for c in range(CHUNKS - 1):
+            for pair in range(2):
+                left_pass(0, c, pair, *wl_first, 2 * P * pair)
         v_words.append(gather_words("v_words1", left_words[1], left_list))
         rounded = [round_weight("wl_v1", wl_raw[1], slice(0, 2), True), scalar_lanes]
         wl_second = [quantize("wl1_%d" % pair, keep, rounded[pair]) for pair in range(2)]
 
-        def maximum(half, t):
-            lo = half * HALF
-            if (half, t) not in early:
-                left_pass(0, half, t, *wl_first, t * P)
-            left_pass(1, half, t, *wl_second[t // 2], (t % 2) * P)
-            if t == 0:
-                stronger[half] = held("stronger%d" % half, [P, PACK, HALF], F32)
-            nc.vector.tensor_tensor(
-                out=stronger[half][:, t, :], in0=a_banks[half, t][:], in1=b_sb[:, t, lo : lo + HALF], op=ALU.max
-            )
+        def maximum(c):
+            half, lo = divmod(c * CHUNK, HALF)
+            stronger[c] = held("stronger%d" % c, [P, PACK, CHUNK], F32)
+            for pair in range(2):
+                if c == CHUNKS - 1:
+                    left_pass(0, c, pair, *wl_first, 2 * P * pair)
+                left_pass(1, c, pair, *wl_second[pair], 0)
+                lanes = slice(2 * pair, 2 * pair + 2)
+                nc.vector.tensor_tensor(
+                    out=stronger[c][:, lanes, :], in0=a_banks[c, pair][:], in1=b_sb[half][:, lanes, lo : lo + CHUNK],
+                    op=ALU.max,
+                )
 
-        def difference(n):
-            c, lo, width = PIECES[n]
-            half, first = divmod(c * CHUNK + lo, HALF)
-            h_rounded[n] = held("h_rounded%d" % n, [P, width, PACK], BF16, "x_rounded3" if n == 0 else "")
-            engine = nc.gpsimd if n == 0 else nc.vector
+        def difference(engine, n, lo, hi):
+            c, first, width = PIECES[n]
+            if lo == 0:
+                h_rounded[n] = held("h_rounded%d" % n, [P, width, PACK], BF16, "x_rounded%d" % (n + 2) if n < 2 else "")
+            cols = slice(first + lo, first + hi)
+            run = RUN if engine is nc.vector else 1
             engine.tensor_tensor(
-                out=h_rounded[n][:].rearrange("p (run i) j -> p run j i", i=RUN),
-                in0=stronger[half][:, :, first : first + width].rearrange("p j (run i) -> p run j i", i=RUN),
-                in1=background[c][:, :, lo : lo + width].rearrange("p j (run i) -> p run j i", i=RUN),
+                out=h_rounded[n][:, lo:hi, :].rearrange("p (run i) j -> p run j i", i=run),
+                in0=stronger[c][:, :, cols].rearrange("p j (run i) -> p run j i", i=run),
+                in1=background[c][:, :, cols].rearrange("p j (run i) -> p run j i", i=run),
                 op=ALU.subtract,
             )
 
@@ -329,25 +334,24 @@ def tile_list_stereo_disparity_scores_kernel(
         round_x(3)
         quantize_x(2)
         activation_of(2)
-        for t in range(PACK):
-            maximum(0, t)
+        maximum(0)
+        difference(nc.gpsimd, 0, 0, CHUNK)
+        maximum(2)
+        maximum(1)
         quantize_x(3)
-        difference(0)
-        for t in range(PACK):
-            maximum(1, t)
         activation_of(3)
-        difference(1)
+        maximum(3)
+        difference(nc.gpsimd, 1, 0, CHUNK // 2)
+        difference(nc.vector, 1, CHUNK // 2, CHUNK)
         quantize_h(0)
         scores(0)
-        vector_gains(2)
-        difference(2)
+        difference(nc.vector, 2, 0, CHUNK)
         quantize_h(1)
         scores(1)
-        vector_gains(3)
-        difference(3)
+        difference(nc.vector, 3, 0, CHUNK // 2)
         quantize_h(2)
         scores(2)
-        difference(4)
+        difference(nc.vector, 4, 0, CHUNK // 2)
         quantize_h(3)
         scores(3)
         quantize_h(4)

@@ -33,6 +33,7 @@ FIRST = 4
 PASS_STEP = 8
 KIB = 1024
 VECTOR_GAINS = [0, 0, 0, 0]
+POOL_SHARE = (224, 96)
 G_BANKS = (6, 7)
 O_BANKS = (2, 3)
 
@@ -116,11 +117,11 @@ def tile_list_stereo_disparity_scores_kernel(
         nc.sync.dma_start(left_list[:], offs)
         load_scales(right_window, tab2_scales)
         load_scales(left_window, tab_scales)
-        wb_raw = held("wb_raw", [P, PACK, H], F32)
-        load_rows(wb_raw[:], wb)
-        x_raw = [at("x_raw0", [P, PACK, HALF], F32, 20 * KIB)]
-        load_rows(x_raw[0][:], x[:, 0:HALF])
+        x_early = held("x_early", [P, PACK, HALF], F32)
+        load_rows(x_early[:], x[:, 0:HALF])
         load_scales(wr_window, wr_scales)
+        wb_raw = at("wb_raw", [P, PACK, H], F32, 20 * KIB)
+        load_rows(wb_raw[:], wb)
         right_words = [held("right_words%d" % a, [P, T], I32, "right_words%d" % a) for a in range(2)]
         load_words(right_words[0][:], tab2_words[0])
         bias = held("bias", [P, PACK], F32)
@@ -151,67 +152,51 @@ def tile_list_stereo_disparity_scores_kernel(
             load_words(left_words[a][:], tab_words[a])
             load_rows(wl_raw[a][:], wl[a * K_PASS : (a + 1) * K_PASS, :])
 
-        x_rounded, x_q, tanhs, background, stronger, h_rounded, h_q = {}, {}, {}, {}, {}, {}, {}
+        x_rounded, x_q, background, stronger, h_rounded, h_q = {}, {}, {}, {}, {}, {}
 
-        def round_x(c):
-            raw = x_raw[0][:, :, c * CHUNK : (c + 1) * CHUNK] if c < 2 else x_late[c - 2][:]
-            x_rounded[c] = held("x_rounded%d" % c, [P, CHUNK, PACK], BF16, "x_rounded%d" % c)
+        def round_x(name, raw, rounded):
+            x_rounded[name] = rounded
             nc.scalar.copy(
-                out=x_rounded[c][:].rearrange("p (run i) j -> p run j i", i=RUN),
-                in_=raw.rearrange("p j (run i) -> p run j i", i=RUN),
+                out=rounded[:].rearrange("p (run i) j -> p run j i", i=RUN),
+                in_=raw[:].rearrange("p j (run i) -> p run j i", i=RUN),
             )
 
-        def quantize_x(c):
-            x_q[c] = quantize("x%d" % c, keep, x_rounded[c][:].rearrange("p col j -> p (col j)"), "b_sb0" if c == 3 else "")
+        def quantize_x(name, tag=""):
+            x_q[name] = quantize("x_" + name, keep, x_rounded[name][:].rearrange("p col j -> p (col j)"), tag)
 
-        g_banks = {}
-
-        def g_product(c, pair):
-            codes, plane = x_q[c]
-            bank = new_bank(G_BANKS[pair // 2], [P, 2, CHUNK])
-            g_banks[c, pair] = bank
-            for e in range(2):
-                nc.tensor.matmul_mx(
-                    out=bank[:, e, :],
-                    lhsT=wb_codes[:, lane(pair + e)].bitcast(FP8X4),
-                    lhsT_scale=wb_plane[:, lane(pair + e)],
-                    rhs=codes[:].bitcast(FP8X4),
-                    rhs_scale=plane[:],
-                    start=True,
-                    stop=True,
-                )
-
-        def activation_of(c):
-            tanhs[c] = ring.tile([P, PACK, CHUNK], F32, name="tanhs", bufs=2)
-            background[c] = held("background%d" % c, [P, PACK, CHUNK], F32)
-            for pair in range(0, PACK, 2):
-                g_product(c, pair)
-                for e in range(2):
-                    t = pair + e
-                    nc.scalar.activation(
-                        out=tanhs[c][:, t, :], in_=g_banks[c, pair][:, e, :], func=ACT.Tanh, bias=bias[:, t : t + 1]
+        def activation_of(name, width):
+            codes, plane = x_q[name]
+            tanhs = held("tanhs_" + name, [P, PACK, width], F32)
+            background[name] = held("background_" + name, [P, PACK, width], F32)
+            together = BANK // width
+            for first in range(0, PACK, together):
+                bank = new_bank(G_BANKS[first // together % 2], [P, together, width])
+                for e in range(together):
+                    wb_codes, wb_plane = wb_q[(first + e) // 2]
+                    nc.tensor.matmul_mx(
+                        out=bank[:, e, :],
+                        lhsT=wb_codes[:, lane((first + e) % 2)].bitcast(FP8X4),
+                        lhsT_scale=wb_plane[:, lane((first + e) % 2)],
+                        rhs=codes[:].bitcast(FP8X4),
+                        rhs_scale=plane[:],
+                        start=True,
+                        stop=True,
                     )
-            for t in range(VECTOR_GAINS[c], PACK):
+                for e in range(together):
+                    t = first + e
+                    nc.scalar.activation(
+                        out=tanhs[:, t, :], in_=bank[:, e, :], func=ACT.Tanh, bias=bias[:, t : t + 1]
+                    )
+            for t in range(PACK):
                 nc.scalar.activation(
-                    out=background[c][:, t, :], in_=tanhs[c][:, t, :], func=ACT.Copy, scale=gains[:, t : t + 1]
+                    out=background[name][:, t, :], in_=tanhs[:, t, :], func=ACT.Copy, scale=gains[:, t : t + 1]
                 )
 
-        def vector_gains(c):
-            for t in range(VECTOR_GAINS[c]):
-                nc.vector.tensor_scalar(
-                    out=background[c][:, t, :], in0=tanhs[c][:, t, :], scalar1=gains[:, t : t + 1], scalar2=None,
-                    op0=ALU.mult,
-                )
-
-        wb_codes, wb_plane = quantize("wb", keep, round_weight("wb_rounded", wb_raw, slice(0, PACK), False))
-        round_x(0)
-        round_x(1)
-        quantize_x(0)
-        activation_of(0)
-        vector_gains(0)
-        quantize_x(1)
-        activation_of(1)
-        vector_gains(1)
+        round_x("early", x_early, held("x_rounded_early", [P, HALF, PACK], BF16))
+        wb_rounded = [round_weight("wb_rounded%d" % u, wb_raw, slice(2 * u, 2 * u + 2), u == 0) for u in range(2)]
+        quantize_x("early")
+        wb_q = [quantize("wb%d" % u, keep, wb_rounded[u]) for u in range(2)]
+        activation_of("early", HALF)
         v2_words = [gather_words("v2_words0", right_words[0], right_list)]
         wr_codes = [held("wr_codes%d" % a, [P, H], I32) for a in range(2)]
         for a in range(2):
@@ -224,7 +209,11 @@ def tile_list_stereo_disparity_scores_kernel(
         load_rows(x_late[0][:], x[:, HALF : HALF + CHUNK])
 
         scalar_lanes = round_weight("wl_s1", wl_raw[1], slice(2, PACK), False)
-        b_sb = [held("b_sb%d" % half, [P, PACK, HALF], F32, "b_sb%d" % half) for half in range(2)]
+        b_sb = {
+            (half, pair): held("b_sb%d%d" % (half, pair), [P, 2, HALF], F32, "b_sb%d%d" % (half, pair))
+            for half in range(2)
+            for pair in range(2)
+        }
         for half in range(2):
             lo = half * HALF
             for t in range(PACK):
@@ -240,7 +229,7 @@ def tile_list_stereo_disparity_scores_kernel(
                         start=(a == 0),
                         stop=(a == 1),
                     )
-                nc.scalar.copy(out=b_sb[half][:, t, :], in_=bank[:])
+                nc.scalar.copy(out=b_sb[half, t // 2][:, t % 2, :], in_=bank[:])
 
         v_words = [gather_words("v_words0", left_words[0], left_list)]
         load_rows(x_late[1][:], x[:, HALF + CHUNK : S])
@@ -281,27 +270,23 @@ def tile_list_stereo_disparity_scores_kernel(
 
         def maximum(c):
             half, lo = divmod(c * CHUNK, HALF)
-            stronger[c] = held("stronger%d" % c, [P, PACK, CHUNK], F32)
             for pair in range(2):
                 if c == CHUNKS - 1:
                     left_pass(0, c, pair, *wl_first, 2 * P * pair)
                 left_pass(1, c, pair, *wl_second[pair], 0)
                 lanes = slice(2 * pair, 2 * pair + 2)
                 nc.vector.tensor_tensor(
-                    out=stronger[c][:, lanes, :], in0=a_banks[c, pair][:], in1=b_sb[half][:, lanes, lo : lo + CHUNK],
+                    out=stronger[c][:, lanes, :], in0=a_banks[c, pair][:], in1=b_sb[half, pair][:, :, lo : lo + CHUNK],
                     op=ALU.max,
                 )
 
         def difference(engine, n, lo, hi):
             c, first, width = PIECES[n]
-            if lo == 0:
-                h_rounded[n] = held("h_rounded%d" % n, [P, width, PACK], BF16, "x_rounded%d" % (n + 2) if n < 2 else "")
             cols = slice(first + lo, first + hi)
-            run = RUN if engine is nc.vector else 1
             engine.tensor_tensor(
-                out=h_rounded[n][:, lo:hi, :].rearrange("p (run i) j -> p run j i", i=run),
-                in0=stronger[c][:, :, cols].rearrange("p j (run i) -> p run j i", i=run),
-                in1=background[c][:, :, cols].rearrange("p j (run i) -> p run j i", i=run),
+                out=h_rounded[n][:, lo:hi, :].rearrange("p (run i) j -> p run j i", i=RUN),
+                in0=stronger[c][:, :, cols].rearrange("p j (run i) -> p run j i", i=RUN),
+                in1=background[c][:, :, cols].rearrange("p j (run i) -> p run j i", i=RUN),
                 op=ALU.subtract,
             )
 
@@ -330,19 +315,32 @@ def tile_list_stereo_disparity_scores_kernel(
                 nc.scalar.copy(out=staged[:], in_=bank[:])
             nc.sync.dma_start(out=out.rearrange("(u p) s -> p u s", p=P)[:, :, first : first + width], in_=staged[:])
 
-        round_x(2)
-        round_x(3)
-        quantize_x(2)
-        activation_of(2)
+        round_x("third", x_late[0], held("x_rounded2", [P, CHUNK, PACK], BF16, "x_rounded2"))
+        round_x("fourth", x_late[1], held("x_rounded3", [P, CHUNK, PACK], BF16, "x_rounded3"))
+        quantize_x("third")
+        activation_of("third", CHUNK)
+        middle = held("stronger_middle", [P, 2, PACK, CHUNK], F32, "right_words1")
+        stronger[1], stronger[2] = middle[:, 0], middle[:, 1]
+        for c in (0, 3):
+            stronger[c] = held("stronger%d" % c, [P, PACK, CHUNK], F32)
+        h_rounded[0] = held("h_rounded0", [P, CHUNK, PACK], BF16, "x_rounded2")
+        h_rounded[1] = held("h_rounded1", [P, CHUNK, PACK], BF16, "x_rounded3")
+        for n in range(2, len(PIECES)):
+            h_rounded[n] = held("h_rounded%d" % n, [P, PIECES[n][2], PACK], BF16)
+        for c in range(2):
+            background[c] = background["early"][:, :, c * CHUNK : (c + 1) * CHUNK]
+        background[2] = background["third"][:]
         maximum(0)
-        difference(nc.gpsimd, 0, 0, CHUNK)
+        difference(nc.gpsimd, 0, 0, POOL_SHARE[0])
         maximum(2)
         maximum(1)
-        quantize_x(3)
-        activation_of(3)
+        quantize_x("fourth", "b_sb00")
+        activation_of("fourth", CHUNK)
+        background[3] = background["fourth"][:]
         maximum(3)
-        difference(nc.gpsimd, 1, 0, CHUNK // 2)
-        difference(nc.vector, 1, CHUNK // 2, CHUNK)
+        difference(nc.gpsimd, 1, 0, POOL_SHARE[1])
+        difference(nc.vector, 0, POOL_SHARE[0], CHUNK)
+        difference(nc.vector, 1, POOL_SHARE[1], CHUNK)
         quantize_h(0)
         scores(0)
         difference(nc.vector, 2, 0, CHUNK)

@@ -31,15 +31,17 @@ RUN = 4
 PIECES = [(0, 0, CHUNK), (1, 0, CHUNK), (2, 0, CHUNK), (3, 0, CHUNK // 2), (3, CHUNK // 2, CHUNK // 2)]
 FIRST = 4
 PASS_STEP = 8
-KIB = 1024
-VECTOR_GAINS = [0, 0, 0, 0]
-POOL_SHARE = (224, 96)
+DISPLACED = 14
+GPSIMD_SHARE = (224, 96)
+A_BANKS = 6
 G_BANKS = (6, 7)
-O_BANKS = (2, 3)
-
-
-def ab_bank(half, t):
-    return (PACK * half + t) % 6
+OUT_BANKS = (2, 3, 4, 5, 0)
+KIB = 1024
+LEFT_WORDS_AT = (0, 16 * KIB)
+WL_RAW_AT = (8 * KIB, 24 * KIB)
+WR_WINDOW_AT = 8 * KIB - H // 2
+WB_RAW_AT = 20 * KIB
+WD_CODES_AT, WD_PLANE_AT, X_LAST_AT = 0, 2 * N, KIB
 
 
 def tile_list_stereo_disparity_scores_kernel(
@@ -106,7 +108,7 @@ def tile_list_stereo_disparity_scores_kernel(
         right_list = held("right_list", [P, S // LIST_ROWS], U16)
         right_window = held("right_window", [P, T // BYTES_I32], I32)
         left_window = held("left_window", [P, T // BYTES_I32], I32)
-        wr_window = at("wr_window", [P, H // BYTES_I32], I32, 8 * KIB - 256)
+        wr_window = at("wr_window", [P, H // BYTES_I32], I32, WR_WINDOW_AT)
         nc.vector.memset(right_window[:], 0)
         nc.vector.memset(left_window[:], 0)
         nc.gpsimd.memset(wr_window[:], 0)
@@ -120,7 +122,7 @@ def tile_list_stereo_disparity_scores_kernel(
         x_early = held("x_early", [P, PACK, HALF], F32)
         load_rows(x_early[:], x[:, 0:HALF])
         load_scales(wr_window, wr_scales)
-        wb_raw = at("wb_raw", [P, PACK, H], F32, 20 * KIB)
+        wb_raw = at("wb_raw", [P, PACK, H], F32, WB_RAW_AT)
         load_rows(wb_raw[:], wb)
         right_words = [held("right_words%d" % a, [P, T], I32, "right_words%d" % a) for a in range(2)]
         load_words(right_words[0][:], tab2_words[0])
@@ -144,10 +146,10 @@ def tile_list_stereo_disparity_scores_kernel(
         for a in range(2):
             for e in range(2):
                 place = FIRST + PASS_STEP * a + 2 + e
-                nc.sync.dma_start(out=settled[place:P:QUAD, :], in_=settled[place + 14 : P : QUAD, :])
+                nc.sync.dma_start(out=settled[place:P:QUAD, :], in_=settled[place + DISPLACED : P : QUAD, :])
 
-        left_words = [at("left_words0", [P, T], I32, 0), at("left_words1", [P, T], I32, 16 * KIB)]
-        wl_raw = [at("wl_raw0", [P, PACK, H], F32, 8 * KIB), at("wl_raw1", [P, PACK, H], F32, 24 * KIB)]
+        left_words = [at("left_words%d" % a, [P, T], I32, LEFT_WORDS_AT[a]) for a in range(2)]
+        wl_raw = [at("wl_raw%d" % a, [P, PACK, H], F32, WL_RAW_AT[a]) for a in range(2)]
         for a in range(2):
             load_words(left_words[a][:], tab_words[a])
             load_rows(wl_raw[a][:], wl[a * K_PASS : (a + 1) * K_PASS, :])
@@ -169,21 +171,21 @@ def tile_list_stereo_disparity_scores_kernel(
             tanhs = held("tanhs_" + name, [P, PACK, width], F32)
             background[name] = held("background_" + name, [P, PACK, width], F32)
             together = BANK // width
-            for first in range(0, PACK, together):
-                bank = new_bank(G_BANKS[first // together % 2], [P, together, width])
+            for lead in range(0, PACK, together):
+                bank = new_bank(G_BANKS[lead // together % 2], [P, together, width])
                 for e in range(together):
-                    wb_codes, wb_plane = wb_q[(first + e) // 2]
+                    wb_codes, wb_plane = wb_q[(lead + e) // 2]
                     nc.tensor.matmul_mx(
                         out=bank[:, e, :],
-                        lhsT=wb_codes[:, lane((first + e) % 2)].bitcast(FP8X4),
-                        lhsT_scale=wb_plane[:, lane((first + e) % 2)],
+                        lhsT=wb_codes[:, lane((lead + e) % 2)].bitcast(FP8X4),
+                        lhsT_scale=wb_plane[:, lane((lead + e) % 2)],
                         rhs=codes[:].bitcast(FP8X4),
                         rhs_scale=plane[:],
                         start=True,
                         stop=True,
                     )
                 for e in range(together):
-                    t = first + e
+                    t = lead + e
                     nc.scalar.activation(
                         out=tanhs[:, t, :], in_=bank[:, e, :], func=ACT.Tanh, bias=bias[:, t : t + 1]
                     )
@@ -197,6 +199,7 @@ def tile_list_stereo_disparity_scores_kernel(
         quantize_x("early")
         wb_q = [quantize("wb%d" % u, keep, wb_rounded[u]) for u in range(2)]
         activation_of("early", HALF)
+
         v2_words = [gather_words("v2_words0", right_words[0], right_list)]
         wr_codes = [held("wr_codes%d" % a, [P, H], I32) for a in range(2)]
         for a in range(2):
@@ -205,7 +208,10 @@ def tile_list_stereo_disparity_scores_kernel(
                 in_=wr_raw[a][:].rearrange("p (m t) -> p t m", t=PACK),
             )
         v2_words.append(gather_words("v2_words1", right_words[1], right_list))
-        x_late = [held("x_raw2", [P, PACK, CHUNK], F32, "right_words1"), at("x_raw3", [P, PACK, CHUNK], F32, KIB)]
+        x_late = [
+            held("x_raw2", [P, PACK, CHUNK], F32, "right_words1"),
+            at("x_raw3", [P, PACK, CHUNK], F32, X_LAST_AT),
+        ]
         load_rows(x_late[0][:], x[:, HALF : HALF + CHUNK])
 
         scalar_lanes = round_weight("wl_s1", wl_raw[1], slice(2, PACK), False)
@@ -219,13 +225,13 @@ def tile_list_stereo_disparity_scores_kernel(
             for t in range(PACK):
                 bank = new_bank(PACK * half + t, [P, BANK])
                 for a in range(2):
-                    first = FIRST + PASS_STEP * a
+                    start_row = FIRST + PASS_STEP * a
                     nc.tensor.matmul_mx(
                         out=bank[:],
                         lhsT=wr_codes[a][:, lane(t)].bitcast(FP8X4),
-                        lhsT_scale=planes[first:, 2 * S + t * P : 2 * S + (t + 1) * P],
+                        lhsT_scale=planes[start_row:, 2 * S + t * P : 2 * S + (t + 1) * P],
                         rhs=v2_words[a][:, lo : lo + HALF].bitcast(FP8X4),
-                        rhs_scale=planes[first:, lo : lo + HALF],
+                        rhs_scale=planes[start_row:, lo : lo + HALF],
                         start=(a == 0),
                         stop=(a == 1),
                     )
@@ -233,8 +239,8 @@ def tile_list_stereo_disparity_scores_kernel(
 
         v_words = [gather_words("v_words0", left_words[0], left_list)]
         load_rows(x_late[1][:], x[:, HALF + CHUNK : S])
-        wd_codes = at("wd_codes", [P, 2 * N], U8, 0)
-        wd_plane = at("wd_plane", [P, N // BYTES_I32], I32, 2 * N)
+        wd_codes = at("wd_codes", [P, 2 * N], U8, WD_CODES_AT)
+        wd_plane = at("wd_plane", [P, N // BYTES_I32], I32, WD_PLANE_AT)
         nc.sync.dma_start(out=wd_codes[:].bitcast(I32), in_=wd_words[0].bitcast(I32))
         nc.gpsimd.memset(wd_plane[:], 0)
         for q in range(P // QUAD):
@@ -248,7 +254,7 @@ def tile_list_stereo_disparity_scores_kernel(
         def left_pass(a, c, pair, codes, plane, column):
             lo = c * CHUNK
             if a == 0:
-                a_banks[c, pair] = new_bank((2 * c + pair) % 6, [P, 2, CHUNK])
+                a_banks[c, pair] = new_bank((2 * c + pair) % A_BANKS, [P, 2, CHUNK])
             for e in range(2):
                 cols = slice(column + e * P, column + (e + 1) * P)
                 nc.tensor.matmul_mx(
@@ -265,8 +271,8 @@ def tile_list_stereo_disparity_scores_kernel(
             for pair in range(2):
                 left_pass(0, c, pair, *wl_first, 2 * P * pair)
         v_words.append(gather_words("v_words1", left_words[1], left_list))
-        rounded = [round_weight("wl_v1", wl_raw[1], slice(0, 2), True), scalar_lanes]
-        wl_second = [quantize("wl1_%d" % pair, keep, rounded[pair]) for pair in range(2)]
+        last_lanes = [round_weight("wl_v1", wl_raw[1], slice(0, 2), True), scalar_lanes]
+        wl_second = [quantize("wl1_%d" % pair, keep, last_lanes[pair]) for pair in range(2)]
 
         def maximum(c):
             half, lo = divmod(c * CHUNK, HALF)
@@ -294,10 +300,10 @@ def tile_list_stereo_disparity_scores_kernel(
             h_q[n] = quantize("h", ring, h_rounded[n][:].rearrange("p col j -> p (col j)"))
 
         def scores(n):
-            c, lo, width = PIECES[n]
-            first = c * CHUNK + lo
+            c, first, width = PIECES[n]
+            lo = c * CHUNK + first
             codes, plane = h_q[n]
-            bank = new_bank(O_BANKS[n % 2], [P, N // P, width])
+            bank = new_bank(OUT_BANKS[n], [P, N // P, width])
             for u in range(N // P):
                 nc.tensor.matmul_mx(
                     out=bank[:, u, :],
@@ -313,7 +319,7 @@ def tile_list_stereo_disparity_scores_kernel(
                 nc.vector.tensor_copy(out=staged[:], in_=bank[:])
             else:
                 nc.scalar.copy(out=staged[:], in_=bank[:])
-            nc.sync.dma_start(out=out.rearrange("(u p) s -> p u s", p=P)[:, :, first : first + width], in_=staged[:])
+            nc.sync.dma_start(out=out.rearrange("(u p) s -> p u s", p=P)[:, :, lo : lo + width], in_=staged[:])
 
         round_x("third", x_late[0], held("x_rounded2", [P, CHUNK, PACK], BF16, "x_rounded2"))
         round_x("fourth", x_late[1], held("x_rounded3", [P, CHUNK, PACK], BF16, "x_rounded3"))
@@ -331,24 +337,24 @@ def tile_list_stereo_disparity_scores_kernel(
             background[c] = background["early"][:, :, c * CHUNK : (c + 1) * CHUNK]
         background[2] = background["third"][:]
         maximum(0)
-        difference(nc.gpsimd, 0, 0, POOL_SHARE[0])
+        difference(nc.gpsimd, 0, 0, GPSIMD_SHARE[0])
         maximum(2)
         maximum(1)
         quantize_x("fourth", "b_sb00")
         activation_of("fourth", CHUNK)
         background[3] = background["fourth"][:]
         maximum(3)
-        difference(nc.gpsimd, 1, 0, POOL_SHARE[1])
-        difference(nc.vector, 0, POOL_SHARE[0], CHUNK)
-        difference(nc.vector, 1, POOL_SHARE[1], CHUNK)
+        difference(nc.gpsimd, 1, 0, GPSIMD_SHARE[1])
+        difference(nc.vector, 0, GPSIMD_SHARE[0], CHUNK)
+        difference(nc.vector, 1, GPSIMD_SHARE[1], CHUNK)
         quantize_h(0)
         scores(0)
         difference(nc.vector, 2, 0, CHUNK)
         quantize_h(1)
         scores(1)
-        difference(nc.vector, 3, 0, CHUNK // 2)
         quantize_h(2)
         scores(2)
+        difference(nc.vector, 3, 0, CHUNK // 2)
         difference(nc.vector, 4, 0, CHUNK // 2)
         quantize_h(3)
         scores(3)

@@ -32,16 +32,17 @@ PIECES = [(0, 0, CHUNK), (1, 0, CHUNK), (2, 0, CHUNK), (3, 0, CHUNK // 2), (3, C
 FIRST = 4
 PASS_STEP = 8
 DISPLACED = 14
-GPSIMD_SHARE = (224, 96)
-A_BANKS = 6
-G_BANKS = (6, 7)
-OUT_BANKS = (2, 3, 4, 5, 0)
+GPSIMD_SHARE = 112
+G_BANKS = {"early": (6, 7), "third": (0, 1), "fourth": (4, 5)}
+OUT_BANKS = (2, 3, 6, 7, 0)
 KIB = 1024
 LEFT_WORDS_AT = (0, 16 * KIB)
 WL_RAW_AT = (8 * KIB, 24 * KIB)
 WR_WINDOW_AT = 8 * KIB - H // 2
 WB_RAW_AT = 20 * KIB
 WD_CODES_AT, WD_PLANE_AT, X_LAST_AT = 0, 2 * N, KIB
+X_ROUNDED_AT = (32 * KIB, 34 * KIB)
+H_ROUNDED_AT = (32 * KIB, 33 * KIB, 31 * KIB)
 
 
 def tile_list_stereo_disparity_scores_kernel(
@@ -172,7 +173,7 @@ def tile_list_stereo_disparity_scores_kernel(
             background[name] = held("background_" + name, [P, PACK, width], F32)
             together = BANK // width
             for lead in range(0, PACK, together):
-                bank = new_bank(G_BANKS[lead // together % 2], [P, together, width])
+                bank = new_bank(G_BANKS[name][lead // together % 2], [P, together, width])
                 for e in range(together):
                     wb_codes, wb_plane = wb_q[(lead + e) // 2]
                     nc.tensor.matmul_mx(
@@ -254,7 +255,7 @@ def tile_list_stereo_disparity_scores_kernel(
         def left_pass(a, c, pair, codes, plane, column):
             lo = c * CHUNK
             if a == 0:
-                a_banks[c, pair] = new_bank((2 * c + pair) % A_BANKS, [P, 2, CHUNK])
+                a_banks[c, pair] = new_bank(2 * c + pair, [P, 2, CHUNK])
             for e in range(2):
                 cols = slice(column + e * P, column + (e + 1) * P)
                 nc.tensor.matmul_mx(
@@ -267,7 +268,7 @@ def tile_list_stereo_disparity_scores_kernel(
                     stop=(a == 1 and e == 1),
                 )
 
-        for c in range(CHUNKS - 1):
+        for c in range(CHUNKS):
             for pair in range(2):
                 left_pass(0, c, pair, *wl_first, 2 * P * pair)
         v_words.append(gather_words("v_words1", left_words[1], left_list))
@@ -277,8 +278,6 @@ def tile_list_stereo_disparity_scores_kernel(
         def maximum(c):
             half, lo = divmod(c * CHUNK, HALF)
             for pair in range(2):
-                if c == CHUNKS - 1:
-                    left_pass(0, c, pair, *wl_first, 2 * P * pair)
                 left_pass(1, c, pair, *wl_second[pair], 0)
                 lanes = slice(2 * pair, 2 * pair + 2)
                 nc.vector.tensor_tensor(
@@ -321,34 +320,33 @@ def tile_list_stereo_disparity_scores_kernel(
                 nc.scalar.copy(out=staged[:], in_=bank[:])
             nc.sync.dma_start(out=out.rearrange("(u p) s -> p u s", p=P)[:, :, lo : lo + width], in_=staged[:])
 
-        round_x("third", x_late[0], held("x_rounded2", [P, CHUNK, PACK], BF16, "x_rounded2"))
-        round_x("fourth", x_late[1], held("x_rounded3", [P, CHUNK, PACK], BF16, "x_rounded3"))
+        round_x("third", x_late[0], at("x_rounded2", [P, CHUNK, PACK], BF16, X_ROUNDED_AT[0]))
+        round_x("fourth", x_late[1], at("x_rounded3", [P, CHUNK, PACK], BF16, X_ROUNDED_AT[1]))
         quantize_x("third")
-        activation_of("third", CHUNK)
         middle = held("stronger_middle", [P, 2, PACK, CHUNK], F32, "right_words1")
         stronger[1], stronger[2] = middle[:, 0], middle[:, 1]
-        for c in (0, 3):
-            stronger[c] = held("stronger%d" % c, [P, PACK, CHUNK], F32)
-        h_rounded[0] = held("h_rounded0", [P, CHUNK, PACK], BF16, "x_rounded2")
-        h_rounded[1] = held("h_rounded1", [P, CHUNK, PACK], BF16, "x_rounded3")
-        for n in range(2, len(PIECES)):
+        stronger[0] = held("stronger0", [P, PACK, CHUNK], F32, "stronger_outer")
+        for n in range(len(H_ROUNDED_AT)):
+            h_rounded[n] = at("h_rounded%d" % n, [P, CHUNK, PACK], BF16, H_ROUNDED_AT[n])
+        for n in range(len(H_ROUNDED_AT), len(PIECES)):
             h_rounded[n] = held("h_rounded%d" % n, [P, PIECES[n][2], PACK], BF16)
         for c in range(2):
             background[c] = background["early"][:, :, c * CHUNK : (c + 1) * CHUNK]
-        background[2] = background["third"][:]
         maximum(0)
-        difference(nc.gpsimd, 0, 0, GPSIMD_SHARE[0])
+        activation_of("third", CHUNK)
+        background[2] = background["third"][:]
+        difference(nc.gpsimd, 0, 0, CHUNK)
         maximum(2)
         maximum(1)
         quantize_x("fourth", "b_sb00")
+        quantize_h(0)
         activation_of("fourth", CHUNK)
         background[3] = background["fourth"][:]
-        maximum(3)
-        difference(nc.gpsimd, 1, 0, GPSIMD_SHARE[1])
-        difference(nc.vector, 0, GPSIMD_SHARE[0], CHUNK)
-        difference(nc.vector, 1, GPSIMD_SHARE[1], CHUNK)
-        quantize_h(0)
         scores(0)
+        stronger[3] = held("stronger3", [P, PACK, CHUNK], F32, "stronger_outer")
+        maximum(3)
+        difference(nc.gpsimd, 1, 0, GPSIMD_SHARE)
+        difference(nc.vector, 1, GPSIMD_SHARE, CHUNK)
         difference(nc.vector, 2, 0, CHUNK)
         quantize_h(1)
         scores(1)

@@ -1,6 +1,7 @@
 from contextlib import ExitStack
 
 import concourse.mybir as mybir
+from concourse.masks import make_identity
 
 K, D, H, N, T, S = 1024, 512, 512, 256, 2048, 1024
 FLOPS = 2 * S * (2 * K * H + D * H + H * N)
@@ -28,13 +29,13 @@ HALF = S // 2
 CHUNK = 256
 CHUNKS = S // CHUNK
 RUN = 4
-PIECES = [(0, 0, CHUNK), (1, 0, CHUNK), (2, 0, CHUNK), (3, 0, CHUNK // 2), (3, CHUNK // 2, CHUNK // 2)]
+TURNED = CHUNK // P
+PIECES = [(0, CHUNK), (CHUNK, CHUNK), (HALF, CHUNK), (HALF + CHUNK, P), (HALF + CHUNK + P, P)]
 FIRST = 4
 PASS_STEP = 8
 DISPLACED = 14
-GPSIMD_SHARE = 112
-G_BANKS = {"early": (6, 7), "third": (0, 1), "fourth": (4, 5)}
-OUT_BANKS = (2, 3, 6, 7, 0)
+G_BANKS = {"early": (6, 7), "third": (0, 1), "fourth": (2, 3)}
+OUT_BANKS = (0, 1, 6, 7, 4)
 KIB = 1024
 LEFT_WORDS_AT = (0, 16 * KIB)
 WL_RAW_AT = (8 * KIB, 24 * KIB)
@@ -42,7 +43,7 @@ WR_WINDOW_AT = 8 * KIB - H // 2
 WB_RAW_AT = 20 * KIB
 WD_CODES_AT, WD_PLANE_AT, X_LAST_AT = 0, 2 * N, KIB
 X_ROUNDED_AT = (32 * KIB, 34 * KIB)
-H_ROUNDED_AT = (32 * KIB, 33 * KIB, 31 * KIB)
+H_ROUNDED_AT = {0: 32 * KIB, 1: 33 * KIB, 3: 33 * KIB, 4: 34 * KIB}
 
 
 def tile_list_stereo_disparity_scores_kernel(
@@ -120,7 +121,7 @@ def tile_list_stereo_disparity_scores_kernel(
         nc.sync.dma_start(left_list[:], offs)
         load_scales(right_window, tab2_scales)
         load_scales(left_window, tab_scales)
-        x_early = held("x_early", [P, PACK, HALF], F32)
+        x_early = held("x_early", [P, PACK, HALF], F32, "x_early")
         load_rows(x_early[:], x[:, 0:HALF])
         load_scales(wr_window, wr_scales)
         wb_raw = at("wb_raw", [P, PACK, H], F32, WB_RAW_AT)
@@ -170,7 +171,7 @@ def tile_list_stereo_disparity_scores_kernel(
         def activation_of(name, width):
             codes, plane = x_q[name]
             tanhs = held("tanhs_" + name, [P, PACK, width], F32)
-            background[name] = held("background_" + name, [P, PACK, width], F32)
+            background[name] = held("background_" + name, [P, PACK, width], F32, "background_" + name)
             together = BANK // width
             for lead in range(0, PACK, together):
                 bank = new_bank(G_BANKS[name][lead // together % 2], [P, together, width])
@@ -216,27 +217,56 @@ def tile_list_stereo_disparity_scores_kernel(
         load_rows(x_late[0][:], x[:, HALF : HALF + CHUNK])
 
         scalar_lanes = round_weight("wl_s1", wl_raw[1], slice(2, PACK), False)
-        b_sb = {
-            (half, pair): held("b_sb%d%d" % (half, pair), [P, 2, HALF], F32, "b_sb%d%d" % (half, pair))
-            for half in range(2)
-            for pair in range(2)
-        }
-        for half in range(2):
-            lo = half * HALF
-            for t in range(PACK):
-                bank = new_bank(PACK * half + t, [P, BANK])
-                for a in range(2):
-                    start_row = FIRST + PASS_STEP * a
+        b_sb = [held("b_sb%d" % pair, [P, 2, HALF], F32, "b_sb%d" % pair) for pair in range(2)]
+        for t in range(PACK):
+            bank = new_bank(t, [P, BANK])
+            for a in range(2):
+                start_row = FIRST + PASS_STEP * a
+                nc.tensor.matmul_mx(
+                    out=bank[:],
+                    lhsT=wr_codes[a][:, lane(t)].bitcast(FP8X4),
+                    lhsT_scale=planes[start_row:, 2 * S + t * P : 2 * S + (t + 1) * P],
+                    rhs=v2_words[a][:, 0:HALF].bitcast(FP8X4),
+                    rhs_scale=planes[start_row:, 0:HALF],
+                    start=(a == 0),
+                    stop=(a == 1),
+                )
+            nc.scalar.copy(out=b_sb[t // 2][:, t % 2, :], in_=bank[:])
+        b_turned = [held("b_turned%d" % i, [P, H], F32, "b_turned%d" % i) for i in range(TURNED)]
+        for i in range(TURNED):
+            lo = HALF + i * P
+            bank = new_bank(PACK + i, [P, BANK])
+            for a in range(2):
+                start_row = FIRST + PASS_STEP * a
+                nc.tensor.matmul_mx(
+                    out=bank[:],
+                    lhsT=v2_words[a][:, lo : lo + P].bitcast(FP8X4),
+                    lhsT_scale=planes[start_row:, lo : lo + P],
+                    rhs=wr_codes[a][:].bitcast(FP8X4),
+                    rhs_scale=planes[start_row:, 2 * S : 2 * S + H],
+                    start=(a == 0),
+                    stop=(a == 1),
+                )
+            nc.scalar.copy(out=b_turned[i][:], in_=bank[:])
+        b_last = [held("b_last%d" % pair, [P, 2, CHUNK], F32) for pair in range(2)]
+        for pair in range(2):
+            bank = new_bank(PACK + TURNED + pair, [P, 2, CHUNK])
+            for a in range(2):
+                start_row = FIRST + PASS_STEP * a
+                for e in range(2):
+                    t = 2 * pair + e
                     nc.tensor.matmul_mx(
-                        out=bank[:],
+                        out=bank[:, e, :],
                         lhsT=wr_codes[a][:, lane(t)].bitcast(FP8X4),
                         lhsT_scale=planes[start_row:, 2 * S + t * P : 2 * S + (t + 1) * P],
-                        rhs=v2_words[a][:, lo : lo + HALF].bitcast(FP8X4),
-                        rhs_scale=planes[start_row:, lo : lo + HALF],
-                        start=(a == 0),
-                        stop=(a == 1),
+                        rhs=v2_words[a][:, S - CHUNK : S].bitcast(FP8X4),
+                        rhs_scale=planes[start_row:, S - CHUNK : S],
+                        start=(a == 0 and e == 0),
+                        stop=(a == 1 and e == 1),
                     )
-                nc.scalar.copy(out=b_sb[half, t // 2][:, t % 2, :], in_=bank[:])
+            nc.scalar.copy(out=b_last[pair][:], in_=bank[:])
+        identity = held("identity", [P, P], F32, "x_early")
+        make_identity(nc, identity[:])
 
         v_words = [gather_words("v_words0", left_words[0], left_list)]
         load_rows(x_late[1][:], x[:, HALF + CHUNK : S])
@@ -268,39 +298,63 @@ def tile_list_stereo_disparity_scores_kernel(
                     stop=(a == 1 and e == 1),
                 )
 
-        for c in range(CHUNKS):
+        def turned_pass(a, i):
+            lo = HALF + i * P
+            if a == 0:
+                a_banks[i] = new_bank(PACK + i, [P, H])
+            parts = [(wl_first, slice(0, H))] if a == 0 else [(wl_second[u], slice(2 * P * u, 2 * P * (u + 1))) for u in range(2)]
+            for (codes, plane), cols in parts:
+                nc.tensor.matmul_mx(
+                    out=a_banks[i][:, cols],
+                    lhsT=v_words[a][:, lo : lo + P].bitcast(FP8X4),
+                    lhsT_scale=planes[FIRST + PASS_STEP * a :, S + lo : S + lo + P],
+                    rhs=codes[:].bitcast(FP8X4),
+                    rhs_scale=plane[:],
+                    start=(a == 0),
+                    stop=(a == 1 and cols.stop == H),
+                )
+
+        for c in range(2):
             for pair in range(2):
                 left_pass(0, c, pair, *wl_first, 2 * P * pair)
+        for i in range(TURNED):
+            turned_pass(0, i)
+        for pair in range(2):
+            left_pass(0, CHUNKS - 1, pair, *wl_first, 2 * P * pair)
         v_words.append(gather_words("v_words1", left_words[1], left_list))
         last_lanes = [round_weight("wl_v1", wl_raw[1], slice(0, 2), True), scalar_lanes]
         wl_second = [quantize("wl1_%d" % pair, keep, last_lanes[pair]) for pair in range(2)]
 
         def maximum(c):
-            half, lo = divmod(c * CHUNK, HALF)
             for pair in range(2):
                 left_pass(1, c, pair, *wl_second[pair], 0)
-                lanes = slice(2 * pair, 2 * pair + 2)
+                right = b_last[pair][:] if c == CHUNKS - 1 else b_sb[pair][:, :, c * CHUNK : (c + 1) * CHUNK]
                 nc.vector.tensor_tensor(
-                    out=stronger[c][:, lanes, :], in0=a_banks[c, pair][:], in1=b_sb[half, pair][:, :, lo : lo + CHUNK],
-                    op=ALU.max,
+                    out=stronger[c][:, 2 * pair : 2 * pair + 2, :], in0=a_banks[c, pair][:], in1=right, op=ALU.max
                 )
 
-        def difference(engine, n, lo, hi):
-            c, first, width = PIECES[n]
-            cols = slice(first + lo, first + hi)
+        def turned_maximum(i):
+            turned_pass(1, i)
+            nc.vector.tensor_tensor(out=turned[:, i, :], in0=a_banks[i][:], in1=b_turned[i][:], op=ALU.max)
+
+        def turn_back(i):
+            turned_back[i] = new_bank(PACK + i, [P, PACK, P])
+            for t in range(PACK):
+                nc.tensor.transpose(turned_back[i][:, t, :], turned[:, i, lane(t)], identity[:])
+
+        def difference(engine, dst, larger, smaller):
             engine.tensor_tensor(
-                out=h_rounded[n][:, lo:hi, :].rearrange("p (run i) j -> p run j i", i=RUN),
-                in0=stronger[c][:, :, cols].rearrange("p j (run i) -> p run j i", i=RUN),
-                in1=background[c][:, :, cols].rearrange("p j (run i) -> p run j i", i=RUN),
+                out=dst.rearrange("p (run i) j -> p run j i", i=RUN),
+                in0=larger.rearrange("p j (run i) -> p run j i", i=RUN),
+                in1=smaller.rearrange("p j (run i) -> p run j i", i=RUN),
                 op=ALU.subtract,
             )
 
-        def quantize_h(n):
-            h_q[n] = quantize("h", ring, h_rounded[n][:].rearrange("p col j -> p (col j)"))
+        def quantize_h(n, tag=""):
+            h_q[n] = quantize("h%d" % n, keep, h_rounded[n][:].rearrange("p col j -> p (col j)"), tag)
 
         def scores(n):
-            c, first, width = PIECES[n]
-            lo = c * CHUNK + first
+            lo, width = PIECES[n]
             codes, plane = h_q[n]
             bank = new_bank(OUT_BANKS[n], [P, N // P, width])
             for u in range(N // P):
@@ -323,38 +377,39 @@ def tile_list_stereo_disparity_scores_kernel(
         round_x("third", x_late[0], at("x_rounded2", [P, CHUNK, PACK], BF16, X_ROUNDED_AT[0]))
         round_x("fourth", x_late[1], at("x_rounded3", [P, CHUNK, PACK], BF16, X_ROUNDED_AT[1]))
         quantize_x("third")
-        middle = held("stronger_middle", [P, 2, PACK, CHUNK], F32, "right_words1")
-        stronger[1], stronger[2] = middle[:, 0], middle[:, 1]
+        turned_back = {}
         stronger[0] = held("stronger0", [P, PACK, CHUNK], F32, "stronger_outer")
-        for n in range(len(H_ROUNDED_AT)):
-            h_rounded[n] = at("h_rounded%d" % n, [P, CHUNK, PACK], BF16, H_ROUNDED_AT[n])
-        for n in range(len(H_ROUNDED_AT), len(PIECES)):
-            h_rounded[n] = held("h_rounded%d" % n, [P, PIECES[n][2], PACK], BF16)
-        for c in range(2):
-            background[c] = background["early"][:, :, c * CHUNK : (c + 1) * CHUNK]
+        later = held("later_maxima", [P, PACK * CHUNK + TURNED * H], F32, "right_words1")
+        stronger[1] = later[:, 0 : PACK * CHUNK].rearrange("p (t e) -> p t e", t=PACK)
+        turned = later[:, PACK * CHUNK :].rearrange("p (i col) -> p i col", i=TURNED)
+        for n, offset in H_ROUNDED_AT.items():
+            h_rounded[n] = at("h_rounded%d" % n, [P, PIECES[n][1], PACK], BF16, offset)
+        h_rounded[2] = held("h_rounded2", [P, CHUNK, PACK], BF16)
+        early = background["early"]
         maximum(0)
         activation_of("third", CHUNK)
-        background[2] = background["third"][:]
-        difference(nc.gpsimd, 0, 0, CHUNK)
-        maximum(2)
+        difference(nc.gpsimd, h_rounded[0][:], stronger[0][:], early[:, :, 0:CHUNK])
+        for i in range(TURNED):
+            turned_maximum(i)
         maximum(1)
-        quantize_x("fourth", "b_sb00")
+        quantize_x("fourth", "b_sb0")
         quantize_h(0)
         activation_of("fourth", CHUNK)
-        background[3] = background["fourth"][:]
         scores(0)
+        difference(nc.gpsimd, h_rounded[1][:], stronger[1], early[:, :, CHUNK:HALF])
         stronger[3] = held("stronger3", [P, PACK, CHUNK], F32, "stronger_outer")
         maximum(3)
-        difference(nc.gpsimd, 1, 0, GPSIMD_SHARE)
-        difference(nc.vector, 1, GPSIMD_SHARE, CHUNK)
-        difference(nc.vector, 2, 0, CHUNK)
+        for i in range(TURNED):
+            turn_back(i)
+        for i in range(TURNED):
+            difference(nc.vector, h_rounded[2][:, lane(i), :], turned_back[i][:], background["third"][:, :, lane(i)])
         quantize_h(1)
+        quantize_h(2, "right_words1")
         scores(1)
-        quantize_h(2)
         scores(2)
-        difference(nc.vector, 3, 0, CHUNK // 2)
-        difference(nc.vector, 4, 0, CHUNK // 2)
+        for i in range(2):
+            difference(nc.vector, h_rounded[3 + i][:], stronger[3][:, :, lane(i)], background["fourth"][:, :, lane(i)])
         quantize_h(3)
-        scores(3)
         quantize_h(4)
+        scores(3)
         scores(4)

@@ -83,14 +83,15 @@ def tile_list_stereo_disparity_scores_kernel(
                 gather(words[:, lo : lo + HALF], window[:].bitcast(U32), offsets, lo, lo + HALF)
             return words
 
-        def round_weight(name, raw, lanes, on_vector):
+        def round_weight(name, raw, lanes, on_vector, steps=1):
             rounded = held(name, [P, lanes.stop - lanes.start, P, PACK], BF16)
-            dst = rounded[:].rearrange("p t m j -> p m j t")
-            src = raw[:].rearrange("p j (m t) -> p m j t", t=PACK)[:, :, :, lanes]
-            if on_vector:
-                nc.vector.tensor_copy(out=dst, in_=src)
-            else:
-                nc.scalar.activation(out=dst, in_=src, func=ACT.Copy)
+            for lo in range(0, P, P // steps):
+                dst = rounded[:].rearrange("p t m j -> p m j t")[:, lo : lo + P // steps]
+                src = raw[:].rearrange("p j (m t) -> p m j t", t=PACK)[:, lo : lo + P // steps, :, lanes]
+                if on_vector:
+                    nc.vector.tensor_copy(out=dst, in_=src)
+                else:
+                    nc.scalar.activation(out=dst, in_=src, func=ACT.Copy)
             return rounded[:].rearrange("p t m j -> p (t m j)")
 
         def quantize(name, pool, rounded, tag=""):
@@ -98,6 +99,17 @@ def tile_list_stereo_disparity_scores_kernel(
             codes = pool.tile([P, width], U32, name=name + "_codes", tag=tag, align_bytes=64)
             plane = pool.tile([P, width], U8, name=name + "_plane", align_bytes=64)
             nc.vector.quantize_mx(out=codes[:].bitcast(FP8X4), scales=plane[:], in_=rounded)
+            return codes, plane
+
+        def quantize_by_halves(name, rounded):
+            codes = held(name + "_codes", [P, 2 * P], U32)
+            plane = held(name + "_plane", [P, 2 * P], U8)
+            for step in range(2):
+                for e in range(2):
+                    lo, hi = e * P + step * P // 2, e * P + (step + 1) * P // 2
+                    nc.vector.quantize_mx(
+                        out=codes[:, lo:hi].bitcast(FP8X4), scales=plane[:, lo:hi], in_=rounded[:, PACK * lo : PACK * hi]
+                    )
             return codes, plane
 
         def new_bank(number, shape):
@@ -216,7 +228,7 @@ def tile_list_stereo_disparity_scores_kernel(
         ]
         load_rows(x_late[0][:], x[:, HALF : HALF + CHUNK])
 
-        scalar_lanes = round_weight("wl_s1", wl_raw[1], slice(2, PACK), False)
+        scalar_lanes = round_weight("wl_s1", wl_raw[1], slice(2, PACK), False, 2)
         b_sb = [held("b_sb%d" % pair, [P, 2, HALF], F32, "b_sb%d" % pair) for pair in range(2)]
         for t in range(PACK):
             bank = new_bank(t, [P, BANK])
@@ -322,8 +334,8 @@ def tile_list_stereo_disparity_scores_kernel(
         for pair in range(2):
             left_pass(0, CHUNKS - 1, pair, *wl_first, 2 * P * pair)
         v_words.append(gather_words("v_words1", left_words[1], left_list))
-        last_lanes = [round_weight("wl_v1", wl_raw[1], slice(0, 2), True), scalar_lanes]
-        wl_second = [quantize("wl1_%d" % pair, keep, last_lanes[pair]) for pair in range(2)]
+        last_lanes = [round_weight("wl_v1", wl_raw[1], slice(0, 2), True, 2), scalar_lanes]
+        wl_second = [quantize_by_halves("wl1_%d" % pair, last_lanes[pair]) for pair in range(2)]
 
         def maximum(c):
             for pair in range(2):

@@ -31,11 +31,12 @@ CHUNKS = S // CHUNK
 RUN = 4
 TURNED = CHUNK // P
 PIECES = [(0, CHUNK), (CHUNK, CHUNK), (HALF, CHUNK), (HALF + CHUNK, P), (HALF + CHUNK + P, P)]
+VECTOR_ROUNDS = 48
 FIRST = 4
 PASS_STEP = 8
 DISPLACED = 14
 G_BANKS = {"early": (6, 7), "third": (0, 1), "fourth": (2, 3)}
-OUT_BANKS = (0, 1, 6, 7, 4)
+OUT_BANKS = ((0,), (1,), (6,), (7, 4), (5, 2))
 KIB = 1024
 LEFT_WORDS_AT = (0, 16 * KIB)
 WL_RAW_AT = (8 * KIB, 24 * KIB)
@@ -170,12 +171,13 @@ def tile_list_stereo_disparity_scores_kernel(
 
         x_rounded, x_q, background, stronger, h_rounded, h_q = {}, {}, {}, {}, {}, {}
 
-        def round_x(name, raw, rounded):
-            x_rounded[name] = rounded
-            nc.scalar.copy(
-                out=rounded[:].rearrange("p (run i) j -> p run j i", i=RUN),
-                in_=raw[:].rearrange("p j (run i) -> p run j i", i=RUN),
-            )
+        def round_x(rounded, raw, on_vector):
+            dst = rounded.rearrange("p (run i) j -> p run j i", i=RUN)
+            src = raw.rearrange("p j (run i) -> p run j i", i=RUN)
+            if on_vector:
+                nc.vector.tensor_copy(out=dst, in_=src)
+            else:
+                nc.scalar.copy(out=dst, in_=src)
 
         def quantize_x(name, tag=""):
             x_q[name] = quantize("x_" + name, keep, x_rounded[name][:].rearrange("p col j -> p (col j)"), tag)
@@ -208,7 +210,8 @@ def tile_list_stereo_disparity_scores_kernel(
                     out=background[name][:, t, :], in_=tanhs[:, t, :], func=ACT.Copy, scale=gains[:, t : t + 1]
                 )
 
-        round_x("early", x_early, held("x_rounded_early", [P, HALF, PACK], BF16))
+        x_rounded["early"] = held("x_rounded_early", [P, HALF, PACK], BF16)
+        round_x(x_rounded["early"][:], x_early[:], False)
         wb_rounded = [round_weight("wb_rounded%d" % u, wb_raw, slice(2 * u, 2 * u + 2), u == 0) for u in range(2)]
         quantize_x("early")
         wb_q = [quantize("wb%d" % u, keep, wb_rounded[u]) for u in range(2)]
@@ -291,7 +294,11 @@ def tile_list_stereo_disparity_scores_kernel(
                 out=wd_plane[QUAD * q : QUAD * q + QUAD_ROWS, :],
                 in_=wd_scales[0, QUAD_ROWS * q : QUAD_ROWS * (q + 1), :].bitcast(I32),
             )
-        wl_first = quantize("wl0", keep, round_weight("wl_v0", wl_raw[0], slice(0, PACK), True))
+        first_lanes = [round_weight("wl_v0_%d" % u, wl_raw[0], slice(2 * u, 2 * u + 2), True) for u in range(2)]
+        wl_first = held("wl0_codes", [P, H], U32), held("wl0_plane", [P, H], U8)
+        for u in range(2):
+            cols = slice(2 * P * u, 2 * P * (u + 1))
+            nc.vector.quantize_mx(out=wl_first[0][:, cols].bitcast(FP8X4), scales=wl_first[1][:, cols], in_=first_lanes[u])
         a_banks = {}
 
         def left_pass(a, c, pair, codes, plane, column):
@@ -368,26 +375,32 @@ def tile_list_stereo_disparity_scores_kernel(
         def scores(n):
             lo, width = PIECES[n]
             codes, plane = h_q[n]
-            bank = new_bank(OUT_BANKS[n], [P, N // P, width])
-            for u in range(N // P):
-                nc.tensor.matmul_mx(
-                    out=bank[:, u, :],
-                    lhsT=wd_codes[:, 2 * P * u : 2 * P * (u + 1)].bitcast(FP4X4),
-                    lhsT_scale=wd_plane[:].bitcast(U8)[:, P * u : P * (u + 1)],
-                    rhs=codes[:].bitcast(FP8X4),
-                    rhs_scale=plane[:],
-                    start=True,
-                    stop=True,
-                )
+            rows = N // P // len(OUT_BANKS[n])
             staged = ring.tile([P, N // P, width], F32, name="staged", bufs=len(PIECES))
-            if n == len(PIECES) - 1:
-                nc.vector.tensor_copy(out=staged[:], in_=bank[:])
-            else:
-                nc.scalar.copy(out=staged[:], in_=bank[:])
+            for which, number in enumerate(OUT_BANKS[n]):
+                bank = new_bank(number, [P, rows, width])
+                for e in range(rows):
+                    u = which * rows + e
+                    nc.tensor.matmul_mx(
+                        out=bank[:, e, :],
+                        lhsT=wd_codes[:, 2 * P * u : 2 * P * (u + 1)].bitcast(FP4X4),
+                        lhsT_scale=wd_plane[:].bitcast(U8)[:, P * u : P * (u + 1)],
+                        rhs=codes[:].bitcast(FP8X4),
+                        rhs_scale=plane[:],
+                        start=True,
+                        stop=True,
+                    )
+                if which == 0:
+                    nc.scalar.copy(out=staged[:, 0:rows, :], in_=bank[:])
+                else:
+                    nc.vector.tensor_copy(out=staged[:, rows:, :], in_=bank[:])
             nc.sync.dma_start(out=out.rearrange("(u p) s -> p u s", p=P)[:, :, lo : lo + width], in_=staged[:])
 
-        round_x("third", x_late[0], at("x_rounded2", [P, CHUNK, PACK], BF16, X_ROUNDED_AT[0]))
-        round_x("fourth", x_late[1], at("x_rounded3", [P, CHUNK, PACK], BF16, X_ROUNDED_AT[1]))
+        x_rounded["third"] = at("x_rounded2", [P, CHUNK, PACK], BF16, X_ROUNDED_AT[0])
+        x_rounded["fourth"] = at("x_rounded3", [P, CHUNK, PACK], BF16, X_ROUNDED_AT[1])
+        round_x(x_rounded["third"][:, :VECTOR_ROUNDS, :], x_late[0][:, :, :VECTOR_ROUNDS], True)
+        round_x(x_rounded["third"][:, VECTOR_ROUNDS:, :], x_late[0][:, :, VECTOR_ROUNDS:], False)
+        round_x(x_rounded["fourth"][:], x_late[1][:], False)
         quantize_x("third")
         turned_back = {}
         stronger[0] = held("stronger0", [P, PACK, CHUNK], F32, "stronger_outer")

from contextlib import ExitStack

import concourse.mybir as mybir
from concourse.masks import make_identity

K, D, H, N, T, S = 1024, 512, 512, 256, 2048, 1024
FLOPS = 2 * S * (2 * K * H + D * H + H * N)

F32 = mybir.dt.float32
BF16 = mybir.dt.bfloat16
I32 = mybir.dt.int32
U32 = mybir.dt.uint32
U16 = mybir.dt.uint16
U8 = mybir.dt.uint8
FP8X4 = mybir.dt.float8_e4m3fn_x4
FP4X4 = mybir.dt.float4_e2m1fn_x4
ALU = mybir.AluOpType
ACT = mybir.ActivationFunctionType

P = 128
PACK = 4
K_PASS = P * PACK
QUAD = 32
QUAD_ROWS = 4
BYTES_I32 = 4
LIST_ROWS = 16
BANK = 512
HALF = S // 2
CHUNK = 256
CHUNKS = S // CHUNK
RUN = 4
TURNED = CHUNK // P
PIECES = [(0, CHUNK), (CHUNK, CHUNK), (HALF, CHUNK), (HALF + CHUNK, P), (HALF + CHUNK + P, P)]
VECTOR_ROUNDS = 48
FIRST = 4
PASS_STEP = 8
DISPLACED = 14
G_BANKS = {"early": (6, 7), "third": (0, 1), "fourth": (2, 3)}
OUT_BANKS = ((0,), (1,), (6,), (7, 4), (5, 2))
KIB = 1024
LEFT_WORDS_AT = (0, 16 * KIB)
WL_RAW_AT = (8 * KIB, 24 * KIB)
WR_WINDOW_AT = 8 * KIB - H // 2
WB_RAW_AT = 20 * KIB
WD_CODES_AT, WD_PLANE_AT, X_LAST_AT = 0, 2 * N, KIB
X_ROUNDED_AT = (32 * KIB, 34 * KIB)
H_ROUNDED_AT = {0: 32 * KIB, 1: 33 * KIB, 3: 33 * KIB, 4: 34 * KIB}


def tile_list_stereo_disparity_scores_kernel(
    tc, tab_words, tab_scales, tab2_words, tab2_scales, offs, offs2, wl, wr_words, wr_scales,
    x, wb, bb, gain, wd_words, wd_scales, out,
):
    nc = tc.nc
    with ExitStack() as ctx:
        keep = ctx.enter_context(tc.tile_pool(name="keep", bufs=1))
        placed = ctx.enter_context(tc.tile_pool(name="placed", bufs=1))
        ring = ctx.enter_context(tc.tile_pool(name="ring", bufs=3))
        psum = ctx.enter_context(tc.psum_pool(name="psum", bufs=1))

        def held(name, shape, dtype, tag=""):
            return keep.tile(shape, dtype, name=name, tag=tag, align_bytes=64)

        def at(name, shape, dtype, offset):
            return placed.tile(shape, dtype, name=name, offset=offset, align_bytes=64)

        def load_scales(window, scales):
            for e in range(2):
                rows = scales[:, e::2, :].rearrange("a w col -> w a col")
                nc.sync.dma_start(out=window[FIRST + e : P : PASS_STEP, :], in_=rows.bitcast(I32))

        def load_words(words, src):
            nc.sync.dma_start(out=words, in_=src.rearrange("p col j -> p (col j)").bitcast(I32))

        def load_rows(raw, rows):
            nc.sync.dma_start(out=raw, in_=rows.rearrange("(p j) col -> p j col", j=PACK))

        def gather(dst, window, offsets, lo, hi):
            nc.vector.tensor_copy(dst, window.indirect(offsets[:, lo // LIST_ROWS : hi // LIST_ROWS]))

        def gather_words(name, window, offsets):
            words = held(name, [P, S], U32)
            for lo in (0, HALF):
                gather(words[:, lo : lo + HALF], window[:].bitcast(U32), offsets, lo, lo + HALF)
            return words

        def round_weight(name, raw, lanes, on_vector, steps=1):
            rounded = held(name, [P, lanes.stop - lanes.start, P, PACK], BF16)
            for lo in range(0, P, P // steps):
                dst = rounded[:].rearrange("p t m j -> p m j t")[:, lo : lo + P // steps]
                src = raw[:].rearrange("p j (m t) -> p m j t", t=PACK)[:, lo : lo + P // steps, :, lanes]
                if on_vector:
                    nc.vector.tensor_copy(out=dst, in_=src)
                else:
                    nc.scalar.activation(out=dst, in_=src, func=ACT.Copy)
            return rounded[:].rearrange("p t m j -> p (t m j)")

        def quantize(name, pool, rounded, tag=""):
            width = rounded.shape[1] // PACK
            codes = pool.tile([P, width], U32, name=name + "_codes", tag=tag, align_bytes=64)
            plane = pool.tile([P, width], U8, name=name + "_plane", align_bytes=64)
            nc.vector.quantize_mx(out=codes[:].bitcast(FP8X4), scales=plane[:], in_=rounded)
            return codes, plane

        def quantize_by_halves(name, rounded):
            codes = held(name + "_codes", [P, 2 * P], U32)
            plane = held(name + "_plane", [P, 2 * P], U8)
            for step in range(2):
                for e in range(2):
                    lo, hi = e * P + step * P // 2, e * P + (step + 1) * P // 2
                    nc.vector.quantize_mx(
                        out=codes[:, lo:hi].bitcast(FP8X4), scales=plane[:, lo:hi], in_=rounded[:, PACK * lo : PACK * hi]
                    )
            return codes, plane

        def new_bank(number, shape):
            return psum.tile(shape, F32, name="bank", tag="bank%d" % number)

        def lane(t):
            return slice(t * P, (t + 1) * P)

        left_list = held("left_list", [P, S // LIST_ROWS], U16)
        right_list = held("right_list", [P, S // LIST_ROWS], U16)
        right_window = held("right_window", [P, T // BYTES_I32], I32)
        left_window = held("left_window", [P, T // BYTES_I32], I32)
        wr_window = at("wr_window", [P, H // BYTES_I32], I32, WR_WINDOW_AT)
        nc.vector.memset(right_window[:], 0)
        nc.vector.memset(left_window[:], 0)
        nc.gpsimd.memset(wr_window[:], 0)

        wr_raw = [held("wr_raw%d" % a, [P, H], I32) for a in range(2)]
        load_words(wr_raw[0][:], wr_words[0])
        nc.sync.dma_start(right_list[:], offs2)
        nc.sync.dma_start(left_list[:], offs)
        load_scales(right_window, tab2_scales)
        load_scales(left_window, tab_scales)
        x_early = held("x_early", [P, PACK, HALF], F32, "x_early")
        load_rows(x_early[:], x[:, 0:HALF])
        load_scales(wr_window, wr_scales)
        wb_raw = at("wb_raw", [P, PACK, H], F32, WB_RAW_AT)
        load_rows(wb_raw[:], wb)
        right_words = [held("right_words%d" % a, [P, T], I32, "right_words%d" % a) for a in range(2)]
        load_words(right_words[0][:], tab2_words[0])
        bias = held("bias", [P, PACK], F32)
        gains = held("gains", [P, PACK], F32)
        nc.sync.dma_start(out=bias[:], in_=bb.rearrange("(p t) -> p t", t=PACK))
        nc.sync.dma_start(out=gains[:], in_=gain.rearrange("(p t) -> p t", t=PACK))
        load_words(wr_raw[1][:], wr_words[1])
        load_words(right_words[1][:], tab2_words[1])

        picked = held("picked", [P, 2 * S], U8)
        gather(picked[:, 0:S], right_window[:].bitcast(U8), right_list, 0, S)
        gather(picked[:, S : 2 * S], left_window[:].bitcast(U8), left_list, 0, S)
        settled = held("settled", [P, (2 * S + H) // BYTES_I32], I32)
        planes = settled[:].bitcast(U8)
        nc.vector.tensor_copy(out=settled[:, 0 : 2 * S // BYTES_I32], in_=picked[:].bitcast(I32))
        nc.vector.tensor_copy(
            out=planes[:, 2 * S : 2 * S + H].rearrange("p (t m) -> p t m", t=PACK),
            in_=wr_window[:].bitcast(U8).rearrange("p (m t) -> p t m", t=PACK),
        )
        for a in range(2):
            for e in range(2):
                place = FIRST + PASS_STEP * a + 2 + e
                nc.sync.dma_start(out=settled[place:P:QUAD, :], in_=settled[place + DISPLACED : P : QUAD, :])

        left_words = [at("left_words%d" % a, [P, T], I32, LEFT_WORDS_AT[a]) for a in range(2)]
        wl_raw = [at("wl_raw%d" % a, [P, PACK, H], F32, WL_RAW_AT[a]) for a in range(2)]
        for a in range(2):
            load_words(left_words[a][:], tab_words[a])
            load_rows(wl_raw[a][:], wl[a * K_PASS : (a + 1) * K_PASS, :])

        x_rounded, x_q, background, stronger, h_rounded, h_q = {}, {}, {}, {}, {}, {}

        def round_x(rounded, raw, on_vector):
            dst = rounded.rearrange("p (run i) j -> p run j i", i=RUN)
            src = raw.rearrange("p j (run i) -> p run j i", i=RUN)
            if on_vector:
                nc.vector.tensor_copy(out=dst, in_=src)
            else:
                nc.scalar.copy(out=dst, in_=src)

        def quantize_x(name, tag=""):
            x_q[name] = quantize("x_" + name, keep, x_rounded[name][:].rearrange("p col j -> p (col j)"), tag)

        def activation_of(name, width):
            codes, plane = x_q[name]
            tanhs = held("tanhs_" + name, [P, PACK, width], F32)
            background[name] = held("background_" + name, [P, PACK, width], F32, "background_" + name)
            together = BANK // width
            for lead in range(0, PACK, together):
                bank = new_bank(G_BANKS[name][lead // together % 2], [P, together, width])
                for e in range(together):
                    wb_codes, wb_plane = wb_q[(lead + e) // 2]
                    nc.tensor.matmul_mx(
                        out=bank[:, e, :],
                        lhsT=wb_codes[:, lane((lead + e) % 2)].bitcast(FP8X4),
                        lhsT_scale=wb_plane[:, lane((lead + e) % 2)],
                        rhs=codes[:].bitcast(FP8X4),
                        rhs_scale=plane[:],
                        start=True,
                        stop=True,
                    )
                for e in range(together):
                    t = lead + e
                    nc.scalar.activation(
                        out=tanhs[:, t, :], in_=bank[:, e, :], func=ACT.Tanh, bias=bias[:, t : t + 1]
                    )
            for t in range(PACK):
                nc.scalar.activation(
                    out=background[name][:, t, :], in_=tanhs[:, t, :], func=ACT.Copy, scale=gains[:, t : t + 1]
                )

        x_rounded["early"] = held("x_rounded_early", [P, HALF, PACK], BF16)
        round_x(x_rounded["early"][:], x_early[:], False)
        wb_rounded = [round_weight("wb_rounded%d" % u, wb_raw, slice(2 * u, 2 * u + 2), u == 0) for u in range(2)]
        quantize_x("early")
        wb_q = [quantize("wb%d" % u, keep, wb_rounded[u]) for u in range(2)]
        activation_of("early", HALF)

        v2_words = [gather_words("v2_words0", right_words[0], right_list)]
        wr_codes = [held("wr_codes%d" % a, [P, H], I32) for a in range(2)]
        for a in range(2):
            nc.gpsimd.tensor_copy(
                out=wr_codes[a][:].rearrange("p (t m) -> p t m", t=PACK),
                in_=wr_raw[a][:].rearrange("p (m t) -> p t m", t=PACK),
            )
        v2_words.append(gather_words("v2_words1", right_words[1], right_list))
        x_late = [
            held("x_raw2", [P, PACK, CHUNK], F32, "right_words1"),
            at("x_raw3", [P, PACK, CHUNK], F32, X_LAST_AT),
        ]
        load_rows(x_late[0][:], x[:, HALF : HALF + CHUNK])

        scalar_lanes = round_weight("wl_s1", wl_raw[1], slice(2, PACK), False, 2)
        b_sb = [held("b_sb%d" % pair, [P, 2, HALF], F32, "b_sb%d" % pair) for pair in range(2)]
        for t in range(PACK):
            bank = new_bank(t, [P, BANK])
            for a in range(2):
                start_row = FIRST + PASS_STEP * a
                nc.tensor.matmul_mx(
                    out=bank[:],
                    lhsT=wr_codes[a][:, lane(t)].bitcast(FP8X4),
                    lhsT_scale=planes[start_row:, 2 * S + t * P : 2 * S + (t + 1) * P],
                    rhs=v2_words[a][:, 0:HALF].bitcast(FP8X4),
                    rhs_scale=planes[start_row:, 0:HALF],
                    start=(a == 0),
                    stop=(a == 1),
                )
            nc.scalar.copy(out=b_sb[t // 2][:, t % 2, :], in_=bank[:])
        b_turned = [held("b_turned%d" % i, [P, H], F32, "b_turned%d" % i) for i in range(TURNED)]
        for i in range(TURNED):
            lo = HALF + i * P
            bank = new_bank(PACK + i, [P, BANK])
            for a in range(2):
                start_row = FIRST + PASS_STEP * a
                nc.tensor.matmul_mx(
                    out=bank[:],
                    lhsT=v2_words[a][:, lo : lo + P].bitcast(FP8X4),
                    lhsT_scale=planes[start_row:, lo : lo + P],
                    rhs=wr_codes[a][:].bitcast(FP8X4),
                    rhs_scale=planes[start_row:, 2 * S : 2 * S + H],
                    start=(a == 0),
                    stop=(a == 1),
                )
            nc.scalar.copy(out=b_turned[i][:], in_=bank[:])
        b_last = [held("b_last%d" % pair, [P, 2, CHUNK], F32) for pair in range(2)]
        for pair in range(2):
            bank = new_bank(PACK + TURNED + pair, [P, 2, CHUNK])
            for a in range(2):
                start_row = FIRST + PASS_STEP * a
                for e in range(2):
                    t = 2 * pair + e
                    nc.tensor.matmul_mx(
                        out=bank[:, e, :],
                        lhsT=wr_codes[a][:, lane(t)].bitcast(FP8X4),
                        lhsT_scale=planes[start_row:, 2 * S + t * P : 2 * S + (t + 1) * P],
                        rhs=v2_words[a][:, S - CHUNK : S].bitcast(FP8X4),
                        rhs_scale=planes[start_row:, S - CHUNK : S],
                        start=(a == 0 and e == 0),
                        stop=(a == 1 and e == 1),
                    )
            nc.scalar.copy(out=b_last[pair][:], in_=bank[:])
        identity = held("identity", [P, P], F32, "x_early")
        make_identity(nc, identity[:])

        v_words = [gather_words("v_words0", left_words[0], left_list)]
        load_rows(x_late[1][:], x[:, HALF + CHUNK : S])
        wd_codes = at("wd_codes", [P, 2 * N], U8, WD_CODES_AT)
        wd_plane = at("wd_plane", [P, N // BYTES_I32], I32, WD_PLANE_AT)
        nc.sync.dma_start(out=wd_codes[:].bitcast(I32), in_=wd_words[0].bitcast(I32))
        nc.gpsimd.memset(wd_plane[:], 0)
        for q in range(P // QUAD):
            nc.sync.dma_start(
                out=wd_plane[QUAD * q : QUAD * q + QUAD_ROWS, :],
                in_=wd_scales[0, QUAD_ROWS * q : QUAD_ROWS * (q + 1), :].bitcast(I32),
            )
        first_lanes = [round_weight("wl_v0_%d" % u, wl_raw[0], slice(2 * u, 2 * u + 2), True) for u in range(2)]
        wl_first = held("wl0_codes", [P, H], U32), held("wl0_plane", [P, H], U8)
        for u in range(2):
            cols = slice(2 * P * u, 2 * P * (u + 1))
            nc.vector.quantize_mx(out=wl_first[0][:, cols].bitcast(FP8X4), scales=wl_first[1][:, cols], in_=first_lanes[u])
        a_banks = {}

        def left_pass(a, c, pair, codes, plane, column):
            lo = c * CHUNK
            if a == 0:
                a_banks[c, pair] = new_bank(2 * c + pair, [P, 2, CHUNK])
            for e in range(2):
                cols = slice(column + e * P, column + (e + 1) * P)
                nc.tensor.matmul_mx(
                    out=a_banks[c, pair][:, e, :],
                    lhsT=codes[:, cols].bitcast(FP8X4),
                    lhsT_scale=plane[:, cols],
                    rhs=v_words[a][:, lo : lo + CHUNK].bitcast(FP8X4),
                    rhs_scale=planes[FIRST + PASS_STEP * a :, S + lo : S + lo + CHUNK],
                    start=(a == 0 and e == 0),
                    stop=(a == 1 and e == 1),
                )

        def turned_pass(a, i):
            lo = HALF + i * P
            if a == 0:
                a_banks[i] = new_bank(PACK + i, [P, H])
            parts = [(wl_first, slice(0, H))] if a == 0 else [(wl_second[u], slice(2 * P * u, 2 * P * (u + 1))) for u in range(2)]
            for (codes, plane), cols in parts:
                nc.tensor.matmul_mx(
                    out=a_banks[i][:, cols],
                    lhsT=v_words[a][:, lo : lo + P].bitcast(FP8X4),
                    lhsT_scale=planes[FIRST + PASS_STEP * a :, S + lo : S + lo + P],
                    rhs=codes[:].bitcast(FP8X4),
                    rhs_scale=plane[:],
                    start=(a == 0),
                    stop=(a == 1 and cols.stop == H),
                )

        for c in range(2):
            for pair in range(2):
                left_pass(0, c, pair, *wl_first, 2 * P * pair)
        for i in range(TURNED):
            turned_pass(0, i)
        for pair in range(2):
            left_pass(0, CHUNKS - 1, pair, *wl_first, 2 * P * pair)
        v_words.append(gather_words("v_words1", left_words[1], left_list))
        last_lanes = [round_weight("wl_v1", wl_raw[1], slice(0, 2), True, 2), scalar_lanes]
        wl_second = [quantize_by_halves("wl1_%d" % pair, last_lanes[pair]) for pair in range(2)]

        def maximum(c):
            for pair in range(2):
                left_pass(1, c, pair, *wl_second[pair], 0)
                right = b_last[pair][:] if c == CHUNKS - 1 else b_sb[pair][:, :, c * CHUNK : (c + 1) * CHUNK]
                nc.vector.tensor_tensor(
                    out=stronger[c][:, 2 * pair : 2 * pair + 2, :], in0=a_banks[c, pair][:], in1=right, op=ALU.max
                )

        def turned_maximum(i):
            turned_pass(1, i)
            nc.vector.tensor_tensor(out=turned[:, i, :], in0=a_banks[i][:], in1=b_turned[i][:], op=ALU.max)

        def turn_back(i):
            turned_back[i] = new_bank(PACK + i, [P, PACK, P])
            for t in range(PACK):
                nc.tensor.transpose(turned_back[i][:, t, :], turned[:, i, lane(t)], identity[:])

        def difference(engine, dst, larger, smaller):
            engine.tensor_tensor(
                out=dst.rearrange("p (run i) j -> p run j i", i=RUN),
                in0=larger.rearrange("p j (run i) -> p run j i", i=RUN),
                in1=smaller.rearrange("p j (run i) -> p run j i", i=RUN),
                op=ALU.subtract,
            )

        def quantize_h(n, tag=""):
            h_q[n] = quantize("h%d" % n, keep, h_rounded[n][:].rearrange("p col j -> p (col j)"), tag)

        def scores(n):
            lo, width = PIECES[n]
            codes, plane = h_q[n]
            rows = N // P // len(OUT_BANKS[n])
            staged = ring.tile([P, N // P, width], F32, name="staged", bufs=len(PIECES))
            for which, number in enumerate(OUT_BANKS[n]):
                bank = new_bank(number, [P, rows, width])
                for e in range(rows):
                    u = which * rows + e
                    nc.tensor.matmul_mx(
                        out=bank[:, e, :],
                        lhsT=wd_codes[:, 2 * P * u : 2 * P * (u + 1)].bitcast(FP4X4),
                        lhsT_scale=wd_plane[:].bitcast(U8)[:, P * u : P * (u + 1)],
                        rhs=codes[:].bitcast(FP8X4),
                        rhs_scale=plane[:],
                        start=True,
                        stop=True,
                    )
                if which == 0:
                    nc.scalar.copy(out=staged[:, 0:rows, :], in_=bank[:])
                else:
                    nc.vector.tensor_copy(out=staged[:, rows:, :], in_=bank[:])
            nc.sync.dma_start(out=out.rearrange("(u p) s -> p u s", p=P)[:, :, lo : lo + width], in_=staged[:])

        x_rounded["third"] = at("x_rounded2", [P, CHUNK, PACK], BF16, X_ROUNDED_AT[0])
        x_rounded["fourth"] = at("x_rounded3", [P, CHUNK, PACK], BF16, X_ROUNDED_AT[1])
        round_x(x_rounded["third"][:, :VECTOR_ROUNDS, :], x_late[0][:, :, :VECTOR_ROUNDS], True)
        round_x(x_rounded["third"][:, VECTOR_ROUNDS:, :], x_late[0][:, :, VECTOR_ROUNDS:], False)
        round_x(x_rounded["fourth"][:], x_late[1][:], False)
        quantize_x("third")
        turned_back = {}
        stronger[0] = held("stronger0", [P, PACK, CHUNK], F32, "stronger_outer")
        later = held("later_maxima", [P, PACK * CHUNK + TURNED * H], F32, "right_words1")
        stronger[1] = later[:, 0 : PACK * CHUNK].rearrange("p (t e) -> p t e", t=PACK)
        turned = later[:, PACK * CHUNK :].rearrange("p (i col) -> p i col", i=TURNED)
        for n, offset in H_ROUNDED_AT.items():
            h_rounded[n] = at("h_rounded%d" % n, [P, PIECES[n][1], PACK], BF16, offset)
        h_rounded[2] = held("h_rounded2", [P, CHUNK, PACK], BF16)
        early = background["early"]
        maximum(0)
        activation_of("third", CHUNK)
        difference(nc.gpsimd, h_rounded[0][:], stronger[0][:], early[:, :, 0:CHUNK])
        for i in range(TURNED):
            turned_maximum(i)
        maximum(1)
        quantize_x("fourth", "b_sb0")
        quantize_h(0)
        activation_of("fourth", CHUNK)
        scores(0)
        difference(nc.gpsimd, h_rounded[1][:], stronger[1], early[:, :, CHUNK:HALF])
        stronger[3] = held("stronger3", [P, PACK, CHUNK], F32, "stronger_outer")
        maximum(3)
        for i in range(TURNED):
            turn_back(i)
        for i in range(TURNED):
            difference(nc.vector, h_rounded[2][:, lane(i), :], turned_back[i][:], background["third"][:, :, lane(i)])
        quantize_h(1)
        quantize_h(2, "right_words1")
        scores(1)
        scores(2)
        for i in range(2):
            difference(nc.vector, h_rounded[3 + i][:], stronger[3][:, :, lane(i)], background["fourth"][:, :, lane(i)])
        quantize_h(3)
        quantize_h(4)
        scores(3)
        scores(4)
